import numpy as np, ml_dtypes
CORES = [48,51,52,55]
N = 4
BF = ml_dtypes.bfloat16
def f(rng, *shape):
    return (rng.standard_normal(shape, dtype=np.float32) * np.exp2(rng.integers(-2, 3, shape[:-1] + (1,)))).astype(BF)
def wide(rng, *shape):
    v = f(rng, *shape).astype(np.float32); k = shape[:-2] + (1, shape[-1])
    return (v * np.exp2(rng.integers(-6, 7, k)) * (rng.random(k) > 0.0625)).astype(BF)
def gentries(a):
    return np.ascontiguousarray(a.reshape(8, 16, -1).transpose(0, 2, 1)).reshape(8, -1)
def gtable(e):
    e = np.asarray(e); return np.ascontiguousarray(e.reshape(8, -1, 16).transpose(0, 2, 1)).reshape(128, -1).astype(np.int32)
Q, CAPP, M, E, D = 256, 80, 3072, 6144, 5
LV, L = [1, 5, 40, 260, 1500], 3000
EMPTY = 2 ** 24 - 1
def cut(rng, n, m, cap, s):
    u = rng.random((m, cap - 1)) + s * rng.random((m, 1))
    return 1 + np.bincount(np.argsort(u.reshape(-1))[:n - m] // (cap - 1), minlength=m)
def tree(rng, lv, n, keys, repeat=False):
    nk = np.sort(rng.integers(0, EMPTY - 16, (16, M)), axis=0) + np.arange(16)[:, None]
    nk[np.arange(16)[:, None] >= rng.integers(1, 17, (1, M))] = EMPTY
    beg = rng.integers(0, E - 15, M); kid = rng.integers(0, M, E)
    ids = np.concatenate([[0], 1 + rng.permutation(M - 1)]); a = np.cumsum([0] + list(lv))
    lev = [ids[a[l]:a[l + 1]] for l in range(D)]; nxt = lev[1:] + [rng.integers(0, M, n) if repeat else rng.permutation(M)[:n]]
    ek = np.asarray(keys); sizes = []
    for l in range(D - 1, -1, -1):
        sz = cut(rng, len(ek), lv[l], 16, 2.0); st = np.cumsum(sz) - sz
        nk[:, lev[l]] = EMPTY; nk[np.arange(len(ek)) - np.repeat(st, sz), np.repeat(lev[l], sz)] = ek
        ek = ek[st]; sizes.insert(0, sz)
    S = np.concatenate(sizes); C = np.concatenate(nxt); t = len(C); m = len(S)
    o = rng.permutation(m); so = S[o]; st = np.zeros(m, np.int64)
    st[o] = np.cumsum(so) - so + np.sort(rng.integers(0, E - 16 - t + 1, m))
    beg[ids[:m]] = st; kid[np.repeat(st - (np.cumsum(S) - S), S) + np.arange(t)] = C
    return nk, beg, kid
def make(rng, shapes=None, ends=False, full=False, alike=False, repeat=False):
    shapes = shapes or [(LV, L)] * N; I = np.int32
    spl = np.sort(rng.integers(0, EMPTY - 16384 * N + 1, (8, N - 1)), axis=1) + 16384 * np.arange(1, N)
    spl = np.concatenate([np.zeros((8, 1), np.int64), spl], axis=1); hi = np.concatenate([spl[:, 1:], np.full((8, 1), EMPTY)], axis=1)
    nk = np.zeros((N, 128, M), I); beg = np.zeros((N, 8, M), I); kid = np.zeros((N, 8, E), I); sk = np.zeros((N, 8, M), np.int64); ln = np.array([n for _, n in shapes])
    for r in range(N):
        lv, n = shapes[r]
        for g in range(8):
            w = int(hi[g, r] - spl[g, r])
            if ends: k = np.arange(n) + (w - n) * (r % 2)
            else: k = np.sort(rng.integers(0, w - n + 1, n)) + np.arange(n)
            k[0] = 0; k = k + spl[g, r]; sk[r, g, :n] = k
            nk[r, 16 * g:16 * g + 16], beg[r, g], kid[r, g] = tree(rng, lv, n, k, repeat)
    q = np.zeros((N, 8, Q), np.int64)
    for r in range(N):
        for g in range(8):
            if full: cn = np.zeros(N, np.int64); cn[rng.permutation(N)] = np.clip(Q - CAPP * np.arange(N), 0, CAPP)
            else: cn = 3 + cut(rng, Q - 3 * N, N, CAPP - 3, 0.5)
            own = np.repeat(np.arange(N), cn); st = np.cumsum(cn) - cn; occ = np.arange(Q) - st[own]
            a = spl[g, own]; b = hi[g, own]; k = sk[own, g, np.floor(rng.random(Q) * ln[own]).astype(np.int64)]
            inside = a + np.floor(rng.random(Q) * (b - a)).astype(np.int64)
            kd = 1 + occ % 4 if ends else np.array([0, 0, 0, 0, 0, 1, 1, 1, 2, 2, 2, 3, 4])[rng.integers(0, 13, Q)]
            v = np.choose(kd, [inside, k, np.maximum(k - 1, a), a, b - 1])
            if alike: v = v[st[own]]
            q[r, g] = v[rng.permutation(Q)]
    return {"nk": nk, "beg": beg, "kid": kid, "vec": f(rng, N, 128, M), "spl": np.stack([spl.astype(I)] * N), "q": np.stack([gtable(x) for x in q])}
def setup_inputs(rng):
    return make(rng)
def setup_inputs_caps(rng):
    return make(rng, full=True)
def setup_inputs_ends(rng):
    return make(rng, ends=True)
def setup_inputs_shapes(rng):
    a = []; n = M
    for l in range(D): n = -(-n // 16); a.insert(0, n)
    k = M * 3 // 8; b = [min(16 ** l, k) for l in range(D)]; s = int(rng.integers(0, 2))
    return make(rng, shapes=[(a, M) if (r + s) % 2 else (b, k) for r in range(N)], repeat=True)
def setup_inputs_alike(rng):
    return make(rng, alike=True)
def setup_inputs_spread(rng):
    d = make(rng); d["vec"] = wide(rng, N, 128, M); return d
def check_inputs(d):
    bad = []; nk, beg, kid, spl, q = [np.asarray(d[x]).astype(np.int64) for x in ("nk", "beg", "kid", "spl", "q")]
    if not np.isfinite(np.asarray(d["vec"]).astype(np.float32)).all(): bad.append("finite")
    if any(bool((a < 0).any() or (a > b).any()) for a, b in ((nk, EMPTY), (beg, E - 16), (kid, M - 1), (spl, EMPTY - 1), (q, EMPTY - 1))): return bad + ["ranges"]
    if (spl != spl[:1]).any() or (spl[:, :, 0] != 0).any() or (np.diff(spl, axis=2) <= 0).any(): return bad + ["splitters"]
    n4 = nk.reshape(N, 8, 16, M)
    if ((n4[:, :, 1:] <= n4[:, :, :-1]) & (n4[:, :, 1:] < EMPTY)).any(): bad.append("nodes")
    ok = True
    for r in range(N):
        for g in range(8):
            nd = np.zeros(1, np.int64); ek = spl[r, g, r:r + 1]; seen = [nd]
            for l in range(D):
                k = n4[r, g][:, nd].T
                if len(nd) > M or (k[:, 0] != ek).any(): ok = False; break
                use = k < EMPTY; ek = k[use]; nd = kid[r, g][(beg[r, g][nd][:, None] + np.arange(16))[use]]
                if l < D - 1:
                    seen.append(nd)
                    if len(nd) > M: ok = False; break
            if not ok: break
            s = np.concatenate(seen); top = spl[r, g, r + 1] if r + 1 < N else EMPTY
            if len(np.unique(s)) != len(s) or (np.diff(ek) <= 0).any() or ek[-1] >= top: ok = False
        if not ok: break
    if not ok: bad.append("tree")
    for r in range(N):
        x = gentries(q[r]); own = np.sum(x[:, :, None] >= spl[r][:, None, :], axis=2) - 1
        if any(np.bincount(own[g], minlength=N).max() > CAPP for g in range(8)): bad.append("caps"); break
    return bad
def reference(nk, beg, kid, vec, spl, q):
    y = np.zeros((N, 128, Q), vec.dtype); G = np.arange(8)[:, None]
    n4 = nk.reshape(N, 8, 16, M); v4 = vec.reshape(N, 8, 16, M)
    for r in range(N):
        x = gentries(q[r])
        own = np.sum(x[:, :, None] >= spl[r][:, None, :], axis=2) - 1
        at = np.zeros((8, Q), np.int64)
        for l in range(D):
            c = np.sum(n4[own, G, :, at] <= x[:, :, None], axis=2)
            at = kid[own, G, beg[own, G, at] + c - 1]
        y[r] = v4[own, G, :, at].transpose(0, 2, 1).reshape(128, Q)
    return {"y": y}

@@ -1,0 +1,335 @@
+from concourse.bass import DstId, RemoteDMATransfer
+from concourse.mybir import AluOpType as A, ActivationFunctionType as AF
+
+CAP = 80
+NS = 4 * CAP
+FILL = 16777214
+
+SCRATCH = {
+    "x": ("sbuf", [128, 256], "int32"),
+    "xq": ("sbuf", [128, 560], "int32"),
+    "ansb": ("sbuf", [128, 560], "bfloat16"),
+    "yb": ("sbuf", [128, 256], "bfloat16"),
+    "nks": ("sbuf", [128, 3072], "int32"),
+    "vecs": ("sbuf", [128, 3072], "bfloat16"),
+    "TB": ("sbuf", [128, 6144], "bfloat16"),
+    "kidc": ("sbuf", [128, 384], "int32"),
+    "begc": ("sbuf", [128, 192], "int32"),
+    "khi": ("sbuf", [128, 384], "bfloat16"),
+    "klo": ("sbuf", [128, 384], "bfloat16"),
+    "bhi": ("sbuf", [128, 192], "bfloat16"),
+    "blo": ("sbuf", [128, 192], "bfloat16"),
+    "Z": ("sbuf", [128, 512], "bfloat16"),
+    "pid": ("sbuf", [128, 8], "int32"),
+    "oi": ("sbuf", [128, 8], "int32"),
+    "gi": ("sbuf", [128, 8], "int32"),
+    "icol": ("sbuf", [128, 8], "float32"),
+    "gcol": ("sbuf", [128, 8], "float32"),
+    "g16": ("sbuf", [128, 8], "float32"),
+    "m0": ("sbuf", [128, 8], "float32"),
+    "m2c": ("sbuf", [128, 8], "float32"),
+    "m4": ("sbuf", [128, 8], "float32"),
+    "mB": ("sbuf", [128, 8], "float32"),
+    "big": ("sbuf", [128, 8], "float32"),
+    "t0": ("sbuf", [128, 8], "float32"),
+    "t1": ("sbuf", [128, 8], "float32"),
+    "dw": ("sbuf", [128, 8], "float32"),
+    "thr": ("sbuf", [128, 8], "float32"),
+    "rootc": ("sbuf", [128, 8], "float32"),
+    "spli": ("sbuf", [128, 8], "int32"),
+    "splf": ("sbuf", [128, 8], "float32"),
+    "row": ("sbuf", [128, 144], "float32"),
+    "dqp": ("sbuf", [128, 128], "float32"),
+    "qg": ("sbuf", [128, 128], "float32"),
+    "selv": ("sbuf", [128, 128], "float32"),
+    "sel": ("sbuf", [128, 128], "float32"),
+    "F": ("sbuf", [128, 144], "bfloat16"),
+    "F4": ("sbuf", [128, 144], "bfloat16"),
+    "FW": ("sbuf", [128, 144], "bfloat16"),
+    "FK": ("sbuf", [128, 144], "bfloat16"),
+    "FB": ("sbuf", [128, 144], "bfloat16"),
+    "F16": ("sbuf", [128, 144], "bfloat16"),
+    "d1": ("sbuf", [128, 128], "bfloat16"),
+    "d2": ("sbuf", [128, 128], "bfloat16"),
+    "Dm": ("sbuf", [128, 128], "bfloat16"),
+    "Ball": ("sbuf", [128, 128], "bfloat16"),
+    "BallB": ("sbuf", [128, 128], "bfloat16"),
+    "R0": ("sbuf", [128, 128], "bfloat16"),
+    "geo": ("sbuf", [128, 256], "bfloat16"),
+    "H": ("sbuf", [128, 256], "bfloat16"),
+    "prod": ("sbuf", [128, 256], "bfloat16"),
+    "posS": ("sbuf", [128, 16], "uint16"),
+    "posG": ("sbuf", [128, 16], "uint16"),
+    "e1": ("sbuf", [128, 16], "uint16"),
+    "ml2": ("sbuf", [128, 16], "uint16"),
+    "e2": ("sbuf", [128, 16], "uint16"),
+    "ml3": ("sbuf", [128, 16], "uint16"),
+    "km": ("sbuf", [128, 16], "bfloat16"),
+    "bm": ("sbuf", [128, 16], "bfloat16"),
+    "kg3": ("sbuf", [128, 256], "bfloat16"),
+    "nk2": ("sbuf", [128, 16], "int32"),
+    "nk3": ("sbuf", [128, 256], "int32"),
+    "bl3": ("sbuf", [128, 256], "bfloat16"),
+}
+for _n in ("s2", "s3", "e3", "n4", "e4", "n5", "e5", "vl"):
+    SCRATCH[_n] = ("sbuf", [128, 20], "uint16")
+for _n in ("ge1", "ge2", "ge3", "ge4", "ge5", "kg4", "kg5", "kg6", "bp3", "bp4", "bp5"):
+    SCRATCH[_n] = ("sbuf", [128, NS], "bfloat16")
+for _n in range(8):
+    SCRATCH["p%d" % _n] = ("psum", [128, 512], "float32")
+
+SEMAPHORES = ["arrx", "arry", "lsx", "lsy", "xl"] + ["e%d" % _k for _k in range(130)]
+
+
+def rank_program(g, core, T, topo):
+    own = T.rank_of(core)
+    if own is None:
+        return
+    N = 4
+    V, S, P, Y = g.vector, g.scalar, g.tensor, g.sync
+    used = [0]
+    done = {"v": {}, "s": {}, "p": {}, "y": {}, "g": {}}
+    names = (("v", V), ("s", S), ("p", P), ("y", Y), ("g", g))
+
+    def ev(inst, n=1):
+        k = "e%d" % used[0]
+        used[0] += 1
+        inst.then_inc(T.sem[k], n)
+        return (k, n)
+
+    def dm(inst):
+        return ev(inst, 16)
+
+    def wait(q, *events):
+        for name, queue in names:
+            if name == q:
+                for k, n in events:
+                    if done[q].get(k, 0) < n:
+                        queue.wait_ge(T.sem[k], n)
+                        done[q][k] = n
+
+    def collect(ps, n, terms):
+        tot = 16 * len(terms)
+        k = 0
+        last = None
+        for fb, rhs, stepped, events in terms:
+            wait("p", *events)
+            for i in range(16):
+                r = rhs[:, i:16 * n:16] if stepped else rhs[:, 16 * i:16 * i + n]
+                last = P.matmul(ps[:, 0:n], fb[:, 16 - i:144 - i], r, k == 0, k == tot - 1)
+                k += 1
+        return ev(last)
+
+    e_spl = dm(Y.dma_start(T.spli[0:32, 0:1], T.spl[:]))
+    for o in range(16):
+        q = Y if o % 2 == 0 else S
+        q.dma_start(T.x[o::16, :], T.q[:]).then_inc(T.sem.xl, 16)
+    e_x = ("xl", 256)
+    e_kid = dm(Y.dma_start(T.kidc[:], T.kid[:]))
+    e_beg = dm(S.dma_start(T.begc[:], T.beg[:]))
+    e_nk = dm(Y.dma_start(T.nks[:], T.nk[:]))
+
+    i_pid = ev(g.iota(T.pid[:, 0:1], [[1, 1]], 0, 1))
+    i_row = ev(g.iota(T.row[:], [[1, 144]], 0, 0, allow_small_or_imprecise_dtypes=True))
+    i_sel = ev(g.iota(T.selv[:], [[-4, 8], [-1, 16]], 0, 1, allow_small_or_imprecise_dtypes=True))
+    i_dqp = ev(g.iota(T.dqp[:], [[1, 128]], 0, -1, allow_small_or_imprecise_dtypes=True))
+    i_qg = ev(g.iota(T.qg[:], [[1, 8], [0, 16]], 0, 0, allow_small_or_imprecise_dtypes=True))
+
+    z = ev(V.memset(T.Z[:], 0.0))
+    f1 = ev(V.memset(T.TB[:, 0:3072], 0.0))
+    wait("s", z)
+    f2 = [ev(S.activation(T.TB[:, c:c + 512], T.Z[:], AF.Copy)) for c in range(3072, 6144, 512)]
+    fx = ev(V.memset(T.xq[:, 240:560], FILL))
+
+    wait("v", i_pid)
+    c_o = ev(V.tensor_scalar(T.oi[:, 0:1], T.pid[:, 0:1], 15, None, A.bitwise_and))
+    c_g = ev(V.tensor_scalar(T.gi[:, 0:1], T.pid[:, 0:1], 4, None, A.arith_shift_right))
+    wait("v", c_o, c_g)
+    c_i = ev(V.tensor_copy(T.icol[:, 0:1], T.oi[:, 0:1]))
+    c_gc = ev(V.tensor_copy(T.gcol[:, 0:1], T.gi[:, 0:1]))
+    c_g16 = ev(V.tensor_scalar(T.g16[:, 0:1], T.gi[:, 0:1], 16.0, 16.0, A.mult, A.add))
+    wait("v", i_sel)
+    c_sel = ev(V.tensor_scalar(T.sel[:], T.selv[:], 0.0, None, A.is_equal))
+    wait("v", c_i, c_g16, i_row)
+    c_F = ev(V.tensor_scalar(T.F[:], T.row[:], T.g16[:, 0:1], None, A.is_equal))
+    delta = 80.0 * ((-own) % N) - 1.0 - 80.0 + (320.0 if own == 0 else 0.0)
+    c_t0 = ev(V.tensor_scalar(T.t0[:, 0:1], T.icol[:, 0:1], float(own), -320.0, A.is_equal, A.mult))
+    c_t1 = ev(V.tensor_scalar(T.t1[:, 0:1], T.icol[:, 0:1], 0.0, delta, A.is_equal, A.mult))
+    c_m4 = ev(V.tensor_scalar(T.m4[:, 0:1], T.icol[:, 0:1], 4.0, None, A.is_lt))
+    c_m2 = ev(V.tensor_scalar(T.m2c[:, 0:1], T.icol[:, 0:1], 2.0, None, A.is_lt))
+    c_m0 = ev(V.tensor_scalar(T.m0[:, 0:1], T.icol[:, 0:1], 0.0, None, A.is_equal))
+    c_big = ev(V.tensor_scalar(T.big[:, 0:1], T.icol[:, 0:1], 4.0, 33554432.0, A.is_ge, A.mult))
+    wait("v", c_t0, c_t1, c_m4, c_m2)
+    c_dw = ev(V.tensor_scalar(T.dw[:, 0:1], T.t1[:, 0:1], T.t0[:, 0:1], 80.0, A.add, A.add))
+    c_mB = ev(V.tensor_tensor(T.mB[:, 0:1], T.m4[:, 0:1], T.m2c[:, 0:1], A.subtract))
+    wait("v", i_dqp)
+    c_d1 = ev(V.tensor_scalar(T.d1[:], T.dqp[:], 0.0, None, A.is_equal))
+    c_d2 = ev(V.tensor_scalar(T.d2[:], T.dqp[:], -1.0, -1.0, A.is_equal, A.mult))
+    wait("v", e_spl)
+    c_sf = ev(V.tensor_copy(T.splf[0:32, 0:1], T.spli[0:32, 0:1]))
+    wait("p", c_sf, c_sel)
+    p_thr = ev(P.matmul(T.p0[:, 0:1], T.sel[0:32, :], T.splf[0:32, 0:1], True, True))
+    wait("v", c_d1, c_d2)
+    c_D = ev(V.tensor_tensor(T.Dm[:], T.d1[:], T.d2[:], A.add))
+    wait("v", i_qg, c_gc)
+    c_B = ev(V.tensor_scalar(T.Ball[:], T.qg[:], T.gcol[:, 0:1], None, A.is_equal))
+    wait("v", p_thr, c_big)
+    c_thr = ev(V.tensor_scalar(T.thr[:, 0:1], T.p0[:, 0:1], T.big[:, 0:1], None, A.add))
+
+    wait("s", c_F, c_dw)
+    c_FW = ev(S.activation(T.FW[:], T.F[:], AF.Identity, scale=T.dw[:, 0:1]))
+    wait("s", c_m4)
+    c_F4 = ev(S.activation(T.F4[:], T.F[:], AF.Identity, scale=T.m4[:, 0:1]))
+    wait("s", c_m2)
+    c_FK = ev(S.activation(T.FK[:], T.F[:], AF.Identity, scale=T.m2c[:, 0:1]))
+    wait("s", c_mB)
+    c_FB = ev(S.activation(T.FB[:], T.F[:], AF.Identity, scale=T.mB[:, 0:1]))
+    c_F16 = ev(S.activation(T.F16[:], T.F[:], AF.Copy, scale=16.0))
+    wait("s", c_B, c_m0)
+    c_R0 = ev(S.activation(T.R0[:], T.Ball[:], AF.Identity, scale=T.m0[:, 0:1]))
+    c_BB = ev(S.activation(T.BallB[:], T.Ball[:], AF.Identity, scale=T.mB[:, 0:1]))
+
+    wait("v", e_x, c_thr)
+    r_ge = ev(V.tensor_scalar(T.geo[:], T.x[:], T.thr[:, 0:1], None, A.is_ge))
+    wait("p", c_D, r_ge)
+    r_oh = ev(P.matmul(T.p1[:, 0:256], T.Dm[:], T.geo[:], True, True))
+    wait("v", e_kid)
+    k_hi = ev(V.tensor_copy(T.khi[:], T.kidc[:]))
+    wait("v", r_oh, z)
+    r_h = ev(V.tensor_tensor_scan(T.H[:], T.p1[:, 0:256], T.Z[:, 0:256], 0.0, A.add, A.add))
+    wait("v", r_h)
+    r_pr = ev(V.tensor_tensor(T.prod[:], T.H[:], T.p1[:, 0:256], A.mult))
+    r_ps = collect(T.p2, 16, [(T.FW, T.geo, True, [c_FW]), (T.F4, T.prod, True, [c_F4, r_pr])])
+    r_pg = collect(T.p3, 16, [(T.FW, T.geo, False, []), (T.F4, T.prod, False, [])])
+    wait("v", k_hi)
+    k_lo = ev(V.tensor_tensor(T.klo[:], T.kidc[:], T.khi[:], A.subtract))
+    wait("v", r_ps)
+    r_pos = ev(V.tensor_copy(T.posS[:], T.p2[:, 0:16]))
+    wait("v", r_pos, fx)
+    r_sc = ev(V.tensor_copy(T.xq[:, 240:560].indirect(T.posS[:, 0:16]), T.x[:]))
+
+    near = [r for r in range(N) if r != own and topo.die(T.cores[r]) == topo.die(core)]
+    far = [r for r in range(N) if r != own and topo.die(T.cores[r]) != topo.die(core)]
+    masks = {}
+    for k, r in enumerate(far):
+        masks[r] = topo.engines(core, T.cores[r])[0::2][4 * k:4 * k + 4]
+    for k, r in enumerate(near):
+        masks[r] = topo.engines(core, T.cores[r])[1::2][4 * k:4 * k + 4]
+
+    def send(buf, sb, db, sem, lsem):
+        tr = []
+        for r in far + near:
+            rid, pid, _s = topo.addr(T.cores[r])
+            a, b = sb(r), db(r)
+            tr.append(RemoteDMATransfer(dst_ids=[DstId(rid=rid, pnc=pid)], dma_engine_mask=sum(1 << e for e in masks[r]),
+                                        remote_sem=sem, src=buf[:, a:a + CAP], dst=buf[:, b:b + CAP]))
+        g.remote_dma_fused(tr, local_sem=lsem)
+
+    wait("g", r_sc)
+    send(T.xq, lambda r: 240 + CAP * ((r - own) % N), lambda r: CAP * ((own - r) % N - 1), T.sem.arrx, T.sem.lsx)
+    a_x = ("arrx", 12)
+
+    wait("v", e_beg)
+    b_hi = ev(V.tensor_copy(T.bhi[:], T.begc[:]))
+    wait("v", b_hi)
+    b_lo = ev(V.tensor_tensor(T.blo[:], T.begc[:], T.bhi[:], A.subtract))
+    wait("y", f1, *f2)
+    wait("y", k_hi, k_lo)
+    t_k = dm(Y.dma_start(T.TB[0::16, :], T.khi[:]))
+    t_l = dm(Y.dma_start(T.TB[1::16, :], T.klo[:]))
+    wait("y", b_hi, b_lo)
+    t_b = dm(Y.dma_start(T.TB[2::16, 0:3072], T.bhi[:]))
+    t_c = dm(Y.dma_start(T.TB[3::16, 0:3072], T.blo[:]))
+    e_vec = dm(Y.dma_start(T.vecs[:], T.vec[:]))
+    tb = [t_k, t_l, t_b, t_c]
+
+    wait("v", r_pg)
+    r_posg = ev(V.tensor_copy(T.posG[:], T.p3[:, 0:16]))
+
+    wait("p", c_R0, b_hi, b_lo)
+    P.matmul(T.p4[:, 0:1], T.R0[:], T.bhi[:, 0:1], True, False)
+    d0 = ev(P.matmul(T.p4[:, 0:1], T.R0[:], T.blo[:, 0:1], False, True))
+    wait("v", d0)
+    d1 = ev(V.tensor_scalar(T.e1[:, 0:1], T.p4[:, 0:1], T.icol[:, 0:1], None, A.add))
+    wait("v", d1, *tb)
+    d2 = ev(V.tensor_copy(T.km[:], T.TB[:].indirect(T.e1[:, 0:1])))
+    d3 = collect(T.p5, 1, [(T.FK, T.km, True, [c_FK, d2])])
+    wait("v", d3)
+    d4 = ev(V.tensor_copy(T.ml2[:, 0:1], T.p5[:, 0:1]))
+    wait("v", d4)
+    d5 = ev(V.tensor_copy(T.bm[:], T.TB[:, 0:3072].indirect(T.ml2[:, 0:1])))
+    wait("p", c_BB, d5)
+    d6 = ev(P.matmul(T.p6[:, 0:16], T.BallB[:], T.bm[:], True, True))
+    wait("v", d6)
+    d7 = ev(V.tensor_scalar(T.e2[:], T.p6[:, 0:16], T.icol[:, 0:1], None, A.add))
+    wait("v", d7)
+    d8 = ev(V.tensor_copy(T.kg3[:, 0:128], T.TB[:].indirect(T.e2[:, 0:8])))
+    wait("s", d7, *tb)
+    d9 = ev(S.activation(T.kg3[:, 128:256], T.TB[:].indirect(T.e2[:, 8:16]), AF.Copy))
+    d10 = collect(T.p4, 16, [(T.FK, T.kg3, True, [d8, d9])])
+    wait("v", e_nk)
+    d11 = ev(V.tensor_copy(T.nk2[:], T.nks[:].indirect(T.ml2[:, 0:1])))
+    c_rt = ev(V.tensor_copy(T.rootc[:, 0:1], T.nks[:, 0:1]))
+    wait("v", d10)
+    d12 = ev(V.tensor_copy(T.ml3[:], T.p4[:, 0:16]))
+    wait("v", d12)
+    d13 = ev(V.tensor_copy(T.nk3[:], T.nks[:].indirect(T.ml3[:])))
+    wait("s", d12)
+    d14 = ev(S.activation(T.bl3[:], T.TB[:, 0:3072].indirect(T.ml3[:]), AF.Copy))
+
+    X = T.xq[:, 0:NS]
+
+    def to_list(buf, ps, event, add):
+        wait("v", event)
+        if add:
+            e = ev(V.tensor_scalar(buf[:], ps[:, 0:20], float(add), None, A.add))
+        else:
+            e = ev(V.tensor_copy(buf[:], ps[:, 0:20]))
+        wait("v", e)
+        return e
+
+    def level(keys, starts, lst, e_lst, ge, bp, ps, deps_v, deps_s):
+        wait("s", e_lst, *deps_s)
+        eb = ev(S.activation(bp[:], starts.indirect(lst[:]), AF.Copy))
+        wait("v", *deps_v)
+        eg = ev(V.tensor_tensor(ge[:], keys.indirect(lst[:]), X, A.is_le))
+        return collect(ps, 20, [(T.FB, bp, True, [c_FB, eb]), (T.F, ge, True, [eg])])
+
+    def child(lst, e_lst, kg, ps):
+        wait("s", e_lst)
+        a = ev(S.activation(kg[:, 160:320], T.TB[:].indirect(lst[:, 10:20]), AF.Copy))
+        b = ev(V.tensor_copy(kg[:, 0:160], T.TB[:].indirect(lst[:, 0:10])))
+        return collect(ps, 20, [(T.FK, kg, True, [a, b])])
+
+    wait("v", a_x, r_sc, c_rt)
+    w1 = ev(V.tensor_scalar(T.ge1[:], X, T.rootc[:, 0:1], None, A.is_ge))
+    q1 = collect(T.p5, 20, [(T.F, T.ge1, True, [c_F, w1])])
+    s2 = to_list(T.s2, T.p5, q1, -1)
+    wait("v", d11)
+    w2 = ev(V.tensor_tensor(T.ge2[:], T.nk2[:].indirect(T.s2[:]), X, A.is_le))
+    q2 = collect(T.p6, 20, [(T.F16, T.ge1, True, [c_F16]), (T.F, T.ge2, True, [w2])])
+    s3 = to_list(T.s3, T.p6, q2, -17)
+    q3 = level(T.nk3[:], T.bl3[:], T.s3, s3, T.ge3, T.bp3, T.p4, [d13], [d14])
+    e3 = to_list(T.e3, T.p4, q3, -1)
+    n4 = to_list(T.n4, T.p5, child(T.e3, e3, T.kg4, T.p5), 0)
+    e4 = to_list(T.e4, T.p6, level(T.nks[:], T.TB[:, 0:3072], T.n4, n4, T.ge4, T.bp4, T.p6, [], []), -1)
+    n5 = to_list(T.n5, T.p4, child(T.e4, e4, T.kg5, T.p4), 0)
+    e5 = to_list(T.e5, T.p5, level(T.nks[:], T.TB[:, 0:3072], T.n5, n5, T.ge5, T.bp5, T.p5, [], []), -1)
+    vl = to_list(T.vl, T.p6, child(T.e5, e5, T.kg6, T.p6), 0)
+
+    wait("v", e_vec)
+    va = ev(V.tensor_copy(T.ansb[:, 0:160], T.vecs[:].indirect(T.vl[:, 0:10])))
+    wait("s", e_vec, vl)
+    vb = ev(S.activation(T.ansb[:, 160:320], T.vecs[:].indirect(T.vl[:, 10:20]), AF.Copy))
+    wait("g", va, vb)
+    send(T.ansb, lambda r: CAP * ((r - own) % N - 1), lambda r: 240 + CAP * ((own - r) % N), T.sem.arry, T.sem.lsy)
+    a_y = ("arry", 12)
+
+    wait("v", a_y, vb, va, r_posg)
+    wait("s", a_y, va, vb, r_posg)
+    y1 = ev(V.tensor_copy(T.yb[:, 0:128], T.ansb[:, 240:560].indirect(T.posG[:, 0:8])))
+    y2 = ev(S.activation(T.yb[:, 128:256], T.ansb[:, 240:560].indirect(T.posG[:, 8:16]), AF.Copy))
+    wait("y", y1, y2)
+    st = dm(Y.dma_start(T.y[:], T.yb[:]))
+    wait("y", st)
+    wait("g", ("lsx", 12), ("lsy", 12))

@@ -4,6 +4,7 @@ from concourse.mybir import AluOpType as A, ActivationFunctionType as AF
 CAP = 80
 NS = 4 * CAP
 FILL = 16777214
+HALF = 2048
 
 SCRATCH = {
     "x": ("sbuf", [128, 256], "int32"),
@@ -19,58 +20,27 @@ SCRATCH = {
     "klo": ("sbuf", [128, 384], "bfloat16"),
     "bhi": ("sbuf", [128, 192], "bfloat16"),
     "blo": ("sbuf", [128, 192], "bfloat16"),
-    "Z": ("sbuf", [128, 512], "bfloat16"),
-    "pid": ("sbuf", [128, 8], "int32"),
-    "oi": ("sbuf", [128, 8], "int32"),
-    "gi": ("sbuf", [128, 8], "int32"),
-    "icol": ("sbuf", [128, 8], "float32"),
-    "gcol": ("sbuf", [128, 8], "float32"),
-    "g16": ("sbuf", [128, 8], "float32"),
-    "m0": ("sbuf", [128, 8], "float32"),
-    "m2c": ("sbuf", [128, 8], "float32"),
-    "m4": ("sbuf", [128, 8], "float32"),
-    "mB": ("sbuf", [128, 8], "float32"),
-    "big": ("sbuf", [128, 8], "float32"),
-    "t0": ("sbuf", [128, 8], "float32"),
-    "t1": ("sbuf", [128, 8], "float32"),
-    "dw": ("sbuf", [128, 8], "float32"),
-    "thr": ("sbuf", [128, 8], "float32"),
-    "rootc": ("sbuf", [128, 8], "float32"),
-    "spli": ("sbuf", [128, 8], "int32"),
-    "splf": ("sbuf", [128, 8], "float32"),
+    "Z": ("sbuf", [128, 256], "bfloat16"),
     "row": ("sbuf", [128, 144], "float32"),
-    "dqp": ("sbuf", [128, 128], "float32"),
     "qg": ("sbuf", [128, 128], "float32"),
-    "selv": ("sbuf", [128, 128], "float32"),
     "sel": ("sbuf", [128, 128], "float32"),
-    "F": ("sbuf", [128, 144], "bfloat16"),
-    "F4": ("sbuf", [128, 144], "bfloat16"),
-    "FW": ("sbuf", [128, 144], "bfloat16"),
-    "FK": ("sbuf", [128, 144], "bfloat16"),
-    "FB": ("sbuf", [128, 144], "bfloat16"),
-    "F16": ("sbuf", [128, 144], "bfloat16"),
-    "d1": ("sbuf", [128, 128], "bfloat16"),
-    "d2": ("sbuf", [128, 128], "bfloat16"),
-    "Dm": ("sbuf", [128, 128], "bfloat16"),
-    "Ball": ("sbuf", [128, 128], "bfloat16"),
-    "BallB": ("sbuf", [128, 128], "bfloat16"),
-    "R0": ("sbuf", [128, 128], "bfloat16"),
-    "geo": ("sbuf", [128, 256], "bfloat16"),
-    "H": ("sbuf", [128, 256], "bfloat16"),
-    "prod": ("sbuf", [128, 256], "bfloat16"),
-    "posS": ("sbuf", [128, 16], "uint16"),
-    "posG": ("sbuf", [128, 16], "uint16"),
-    "e1": ("sbuf", [128, 16], "uint16"),
-    "ml2": ("sbuf", [128, 16], "uint16"),
-    "e2": ("sbuf", [128, 16], "uint16"),
-    "ml3": ("sbuf", [128, 16], "uint16"),
     "km": ("sbuf", [128, 16], "bfloat16"),
     "bm": ("sbuf", [128, 16], "bfloat16"),
-    "kg3": ("sbuf", [128, 256], "bfloat16"),
     "nk2": ("sbuf", [128, 16], "int32"),
     "nk3": ("sbuf", [128, 256], "int32"),
-    "bl3": ("sbuf", [128, 256], "bfloat16"),
 }
+for _n in ("pid", "pidw", "wi", "oi", "gi", "spli"):
+    SCRATCH[_n] = ("sbuf", [128, 8], "int32")
+for _n in ("w", "icol", "gcol", "g16", "m0", "m2c", "m4", "mB", "big", "thr", "rootc", "splf"):
+    SCRATCH[_n] = ("sbuf", [128, 8], "float32")
+for _n in ("F", "F4", "FK", "FB", "F16"):
+    SCRATCH[_n] = ("sbuf", [128, 144], "bfloat16")
+for _n in ("Dm", "Ball", "BallB", "R0"):
+    SCRATCH[_n] = ("sbuf", [128, 128], "bfloat16")
+for _n in ("geo", "H", "prod", "kg3", "bl3"):
+    SCRATCH[_n] = ("sbuf", [128, 256], "bfloat16")
+for _n in ("posS", "posG", "e1", "ml2", "e2", "ml3"):
+    SCRATCH[_n] = ("sbuf", [128, 16], "uint16")
 for _n in ("s2", "s3", "e3", "n4", "e4", "n5", "e5", "vl"):
     SCRATCH[_n] = ("sbuf", [128, 20], "uint16")
 for _n in ("ge1", "ge2", "ge3", "ge4", "ge5", "kg4", "kg5", "kg6", "bp3", "bp4", "bp5"):
@@ -78,7 +48,7 @@ for _n in ("ge1", "ge2", "ge3", "ge4", "ge5", "kg4", "kg5", "kg6", "bp3", "bp4",
 for _n in range(8):
     SCRATCH["p%d" % _n] = ("psum", [128, 512], "float32")
 
-SEMAPHORES = ["arrx", "arry", "lsx", "lsy", "xl"] + ["e%d" % _k for _k in range(130)]
+SEMAPHORES = ["arrx", "arry", "lsx", "lsy", "xl", "sent"] + ["e%d" % _k for _k in range(130)]
 
 
 def rank_program(g, core, T, topo):
@@ -120,74 +90,60 @@ def rank_program(g, core, T, topo):
                 k += 1
         return ev(last)
 
+    e_beg = dm(S.dma_start(T.begc[:], T.beg[:]))
     e_spl = dm(Y.dma_start(T.spli[0:32, 0:1], T.spl[:]))
     for o in range(16):
         q = Y if o % 2 == 0 else S
         q.dma_start(T.x[o::16, :], T.q[:]).then_inc(T.sem.xl, 16)
     e_x = ("xl", 256)
     e_kid = dm(Y.dma_start(T.kidc[:], T.kid[:]))
-    e_beg = dm(S.dma_start(T.begc[:], T.beg[:]))
-    e_nk = dm(Y.dma_start(T.nks[:], T.nk[:]))
+    e_nk = [dm(Y.dma_start(T.nks[:, 0:HALF], T.nk[:, 0:HALF]))]
 
+    z = ev(V.memset(T.Dm[:], 0.0))
+    z2 = ev(V.memset(T.sel[0:32, :], 0.0))
+    f1 = ev(V.memset(T.TB[:, 0:1536], 0.0))
     i_pid = ev(g.iota(T.pid[:, 0:1], [[1, 1]], 0, 1))
+    i_pw = ev(g.iota(T.pidw[:, 0:1], [[1, 1]], N - own, 1))
     i_row = ev(g.iota(T.row[:], [[1, 144]], 0, 0, allow_small_or_imprecise_dtypes=True))
-    i_sel = ev(g.iota(T.selv[:], [[-4, 8], [-1, 16]], 0, 1, allow_small_or_imprecise_dtypes=True))
-    i_dqp = ev(g.iota(T.dqp[:], [[1, 128]], 0, -1, allow_small_or_imprecise_dtypes=True))
+    wait("g", z2)
+    c_sel = ev(g.affine_select(T.sel[0:32, :], T.sel[0:32, :], [[-4, 8], [-1, 16]], A.not_equal, 1.0, 0, 1))
+    wait("g", z)
+    c_d1 = ev(g.affine_select(T.Dm[:], T.Dm[:], [[-1, 128]], A.not_equal, 1.0, 0, 1))
+    wait("g", c_d1)
+    c_D = ev(g.affine_select(T.Dm[:], T.Dm[:], [[-1, 128]], A.not_equal, -1.0, -1, 1))
+    fx = ev(g.iota(T.xq[:, 240:560], [[0, 320]], FILL, 0))
     i_qg = ev(g.iota(T.qg[:], [[1, 8], [0, 16]], 0, 0, allow_small_or_imprecise_dtypes=True))
+    f4 = ev(g.iota(T.TB[:, 5632:6144], [[0, 512]], 0, 0, allow_small_or_imprecise_dtypes=True))
 
-    z = ev(V.memset(T.Z[:], 0.0))
-    f1 = ev(V.memset(T.TB[:, 0:3072], 0.0))
-    wait("s", z)
-    f2 = [ev(S.activation(T.TB[:, c:c + 512], T.Z[:], AF.Copy)) for c in range(3072, 6144, 512)]
-    fx = ev(V.memset(T.xq[:, 240:560], FILL))
-
-    wait("v", i_pid)
+    zs = ev(V.memset(T.Z[:], 0.0))
+    wait("v", i_pid, i_pw)
     c_o = ev(V.tensor_scalar(T.oi[:, 0:1], T.pid[:, 0:1], 15, None, A.bitwise_and))
     c_g = ev(V.tensor_scalar(T.gi[:, 0:1], T.pid[:, 0:1], 4, None, A.arith_shift_right))
-    wait("v", c_o, c_g)
-    c_i = ev(V.tensor_copy(T.icol[:, 0:1], T.oi[:, 0:1]))
-    c_gc = ev(V.tensor_copy(T.gcol[:, 0:1], T.gi[:, 0:1]))
+    c_wi = ev(V.tensor_scalar(T.wi[:, 0:1], T.pidw[:, 0:1], 3, None, A.bitwise_and))
+    wait("v", c_o, c_g, c_wi)
     c_g16 = ev(V.tensor_scalar(T.g16[:, 0:1], T.gi[:, 0:1], 16.0, 16.0, A.mult, A.add))
-    wait("v", i_sel)
-    c_sel = ev(V.tensor_scalar(T.sel[:], T.selv[:], 0.0, None, A.is_equal))
-    wait("v", c_i, c_g16, i_row)
+    c_m4 = ev(V.tensor_scalar(T.m4[:, 0:1], T.oi[:, 0:1], 4.0, None, A.is_lt))
+    c_big = ev(V.tensor_scalar(T.big[:, 0:1], T.oi[:, 0:1], 4.0, 33554432.0, A.is_ge, A.mult))
+    c_w = ev(V.tensor_scalar(T.w[:, 0:1], T.wi[:, 0:1], 80.0, -161.0, A.mult, A.add))
+    wait("v", c_g16, i_row)
     c_F = ev(V.tensor_scalar(T.F[:], T.row[:], T.g16[:, 0:1], None, A.is_equal))
-    delta = 80.0 * ((-own) % N) - 1.0 - 80.0 + (320.0 if own == 0 else 0.0)
-    c_t0 = ev(V.tensor_scalar(T.t0[:, 0:1], T.icol[:, 0:1], float(own), -320.0, A.is_equal, A.mult))
-    c_t1 = ev(V.tensor_scalar(T.t1[:, 0:1], T.icol[:, 0:1], 0.0, delta, A.is_equal, A.mult))
-    c_m4 = ev(V.tensor_scalar(T.m4[:, 0:1], T.icol[:, 0:1], 4.0, None, A.is_lt))
-    c_m2 = ev(V.tensor_scalar(T.m2c[:, 0:1], T.icol[:, 0:1], 2.0, None, A.is_lt))
-    c_m0 = ev(V.tensor_scalar(T.m0[:, 0:1], T.icol[:, 0:1], 0.0, None, A.is_equal))
-    c_big = ev(V.tensor_scalar(T.big[:, 0:1], T.icol[:, 0:1], 4.0, 33554432.0, A.is_ge, A.mult))
-    wait("v", c_t0, c_t1, c_m4, c_m2)
-    c_dw = ev(V.tensor_scalar(T.dw[:, 0:1], T.t1[:, 0:1], T.t0[:, 0:1], 80.0, A.add, A.add))
-    c_mB = ev(V.tensor_tensor(T.mB[:, 0:1], T.m4[:, 0:1], T.m2c[:, 0:1], A.subtract))
-    wait("v", i_dqp)
-    c_d1 = ev(V.tensor_scalar(T.d1[:], T.dqp[:], 0.0, None, A.is_equal))
-    c_d2 = ev(V.tensor_scalar(T.d2[:], T.dqp[:], -1.0, -1.0, A.is_equal, A.mult))
     wait("v", e_spl)
     c_sf = ev(V.tensor_copy(T.splf[0:32, 0:1], T.spli[0:32, 0:1]))
     wait("p", c_sf, c_sel)
     p_thr = ev(P.matmul(T.p0[:, 0:1], T.sel[0:32, :], T.splf[0:32, 0:1], True, True))
-    wait("v", c_d1, c_d2)
-    c_D = ev(V.tensor_tensor(T.Dm[:], T.d1[:], T.d2[:], A.add))
-    wait("v", i_qg, c_gc)
-    c_B = ev(V.tensor_scalar(T.Ball[:], T.qg[:], T.gcol[:, 0:1], None, A.is_equal))
     wait("v", p_thr, c_big)
     c_thr = ev(V.tensor_scalar(T.thr[:, 0:1], T.p0[:, 0:1], T.big[:, 0:1], None, A.add))
+    wait("v", e_beg)
+    b_hi = ev(V.tensor_copy(T.bhi[:], T.begc[:]))
+    wait("v", b_hi)
+    b_lo = ev(V.tensor_tensor(T.blo[:], T.begc[:], T.bhi[:], A.subtract))
 
-    wait("s", c_F, c_dw)
-    c_FW = ev(S.activation(T.FW[:], T.F[:], AF.Identity, scale=T.dw[:, 0:1]))
-    wait("s", c_m4)
+    wait("s", f1)
+    f2 = [ev(S.activation(T.TB[:, 1536:3072], T.TB[:, 0:1536], AF.Copy))]
+    wait("s", c_F, c_m4)
     c_F4 = ev(S.activation(T.F4[:], T.F[:], AF.Identity, scale=T.m4[:, 0:1]))
-    wait("s", c_m2)
-    c_FK = ev(S.activation(T.FK[:], T.F[:], AF.Identity, scale=T.m2c[:, 0:1]))
-    wait("s", c_mB)
-    c_FB = ev(S.activation(T.FB[:], T.F[:], AF.Identity, scale=T.mB[:, 0:1]))
-    c_F16 = ev(S.activation(T.F16[:], T.F[:], AF.Copy, scale=16.0))
-    wait("s", c_B, c_m0)
-    c_R0 = ev(S.activation(T.R0[:], T.Ball[:], AF.Identity, scale=T.m0[:, 0:1]))
-    c_BB = ev(S.activation(T.BallB[:], T.Ball[:], AF.Identity, scale=T.mB[:, 0:1]))
+    f2.append(ev(S.activation(T.TB[:, 3072:4608], T.TB[:, 0:1536], AF.Copy)))
+    f2.append(ev(S.activation(T.TB[:, 4608:5632], T.TB[:, 0:1024], AF.Copy)))
 
     wait("v", e_x, c_thr)
     r_ge = ev(V.tensor_scalar(T.geo[:], T.x[:], T.thr[:, 0:1], None, A.is_ge))
@@ -195,18 +151,35 @@ def rank_program(g, core, T, topo):
     r_oh = ev(P.matmul(T.p1[:, 0:256], T.Dm[:], T.geo[:], True, True))
     wait("v", e_kid)
     k_hi = ev(V.tensor_copy(T.khi[:], T.kidc[:]))
-    wait("v", r_oh, z)
-    r_h = ev(V.tensor_tensor_scan(T.H[:], T.p1[:, 0:256], T.Z[:, 0:256], 0.0, A.add, A.add))
+    wait("v", r_oh, zs, c_w)
+    r_h = ev(V.tensor_tensor_scan(T.H[:], T.p1[:, 0:256], T.Z[:], T.w[:, 0:1], A.add, A.add))
     wait("v", r_h)
     r_pr = ev(V.tensor_tensor(T.prod[:], T.H[:], T.p1[:, 0:256], A.mult))
-    r_ps = collect(T.p2, 16, [(T.FW, T.geo, True, [c_FW]), (T.F4, T.prod, True, [c_F4, r_pr])])
-    r_pg = collect(T.p3, 16, [(T.FW, T.geo, False, []), (T.F4, T.prod, False, [])])
+    r_ps = collect(T.p2, 16, [(T.F4, T.prod, True, [c_F4, r_pr])])
+    r_pg = collect(T.p3, 16, [(T.F4, T.prod, False, [])])
     wait("v", k_hi)
     k_lo = ev(V.tensor_tensor(T.klo[:], T.kidc[:], T.khi[:], A.subtract))
     wait("v", r_ps)
-    r_pos = ev(V.tensor_copy(T.posS[:], T.p2[:, 0:16]))
+    r_pos = ev(V.tensor_scalar(T.posS[:], T.p2[:, 0:16], 160.0, None, A.add))
     wait("v", r_pos, fx)
     r_sc = ev(V.tensor_copy(T.xq[:, 240:560].indirect(T.posS[:, 0:16]), T.x[:]))
+
+    wait("v", i_qg)
+    c_i = ev(V.tensor_copy(T.icol[:, 0:1], T.oi[:, 0:1]))
+    c_gc = ev(V.tensor_copy(T.gcol[:, 0:1], T.gi[:, 0:1]))
+    c_m2 = ev(V.tensor_scalar(T.m2c[:, 0:1], T.oi[:, 0:1], 2.0, None, A.is_lt))
+    c_m0 = ev(V.tensor_scalar(T.m0[:, 0:1], T.oi[:, 0:1], 0.0, None, A.is_equal))
+    wait("v", c_gc, c_m4, c_m2, c_i)
+    c_B = ev(V.tensor_scalar(T.Ball[:], T.qg[:], T.gcol[:, 0:1], None, A.is_equal))
+    c_mB = ev(V.tensor_tensor(T.mB[:, 0:1], T.m4[:, 0:1], T.m2c[:, 0:1], A.subtract))
+    wait("s", c_B, c_m0)
+    c_R0 = ev(S.activation(T.R0[:], T.Ball[:], AF.Identity, scale=T.m0[:, 0:1]))
+    wait("s", c_m2)
+    c_FK = ev(S.activation(T.FK[:], T.F[:], AF.Identity, scale=T.m2c[:, 0:1]))
+    wait("s", c_mB)
+    c_BB = ev(S.activation(T.BallB[:], T.Ball[:], AF.Identity, scale=T.mB[:, 0:1]))
+    c_F16 = ev(S.activation(T.F16[:], T.F[:], AF.Copy, scale=16.0))
+    c_FB = ev(S.activation(T.FB[:], T.F[:], AF.Identity, scale=T.mB[:, 0:1]))
 
     near = [r for r in range(N) if r != own and topo.die(T.cores[r]) == topo.die(core)]
     far = [r for r in range(N) if r != own and topo.die(T.cores[r]) != topo.die(core)]
@@ -228,24 +201,23 @@ def rank_program(g, core, T, topo):
     wait("g", r_sc)
     send(T.xq, lambda r: 240 + CAP * ((r - own) % N), lambda r: CAP * ((own - r) % N - 1), T.sem.arrx, T.sem.lsx)
     a_x = ("arrx", 12)
+    g.sem_inc(T.sem.sent, 1)
 
-    wait("v", e_beg)
-    b_hi = ev(V.tensor_copy(T.bhi[:], T.begc[:]))
-    wait("v", b_hi)
-    b_lo = ev(V.tensor_tensor(T.blo[:], T.begc[:], T.bhi[:], A.subtract))
-    wait("y", f1, *f2)
+    wait("y", b_hi, b_lo, f1, f4, *f2)
+    t_b = dm(Y.dma_start(T.TB[2::16, 0:3072], T.bhi[:]))
+    t_c = dm(Y.dma_start(T.TB[3::16, 0:3072], T.blo[:]))
     wait("y", k_hi, k_lo)
     t_k = dm(Y.dma_start(T.TB[0::16, :], T.khi[:]))
     t_l = dm(Y.dma_start(T.TB[1::16, :], T.klo[:]))
-    wait("y", b_hi, b_lo)
-    t_b = dm(Y.dma_start(T.TB[2::16, 0:3072], T.bhi[:]))
-    t_c = dm(Y.dma_start(T.TB[3::16, 0:3072], T.blo[:]))
+    wait("y", ("sent", 1))
+    e_nk.append(dm(Y.dma_start(T.nks[:, HALF:3072], T.nk[:, HALF:3072])))
     e_vec = dm(Y.dma_start(T.vecs[:], T.vec[:]))
     tb = [t_k, t_l, t_b, t_c]
 
     wait("v", r_pg)
-    r_posg = ev(V.tensor_copy(T.posG[:], T.p3[:, 0:16]))
+    r_posg = ev(V.tensor_scalar(T.posG[:], T.p3[:, 0:16], 160.0, None, A.add))
 
+    X = T.xq[:, 0:NS]
     wait("p", c_R0, b_hi, b_lo)
     P.matmul(T.p4[:, 0:1], T.R0[:], T.bhi[:, 0:1], True, False)
     d0 = ev(P.matmul(T.p4[:, 0:1], T.R0[:], T.blo[:, 0:1], False, True))
@@ -267,17 +239,12 @@ def rank_program(g, core, T, topo):
     wait("s", d7, *tb)
     d9 = ev(S.activation(T.kg3[:, 128:256], T.TB[:].indirect(T.e2[:, 8:16]), AF.Copy))
     d10 = collect(T.p4, 16, [(T.FK, T.kg3, True, [d8, d9])])
-    wait("v", e_nk)
-    d11 = ev(V.tensor_copy(T.nk2[:], T.nks[:].indirect(T.ml2[:, 0:1])))
+    wait("v", e_nk[0])
     c_rt = ev(V.tensor_copy(T.rootc[:, 0:1], T.nks[:, 0:1]))
     wait("v", d10)
     d12 = ev(V.tensor_copy(T.ml3[:], T.p4[:, 0:16]))
-    wait("v", d12)
-    d13 = ev(V.tensor_copy(T.nk3[:], T.nks[:].indirect(T.ml3[:])))
     wait("s", d12)
     d14 = ev(S.activation(T.bl3[:], T.TB[:, 0:3072].indirect(T.ml3[:]), AF.Copy))
-
-    X = T.xq[:, 0:NS]
 
     def to_list(buf, ps, event, add):
         wait("v", event)
@@ -290,10 +257,11 @@ def rank_program(g, core, T, topo):
 
     def level(keys, starts, lst, e_lst, ge, bp, ps, deps_v, deps_s):
         wait("s", e_lst, *deps_s)
-        eb = ev(S.activation(bp[:], starts.indirect(lst[:]), AF.Copy))
-        wait("v", *deps_v)
+        ea = ev(S.activation(bp[:, 0:192], starts.indirect(lst[:, 0:12]), AF.Copy))
+        wait("v", *deps_v, *deps_s)
+        eb = ev(V.tensor_copy(bp[:, 192:320], starts.indirect(lst[:, 12:20])))
         eg = ev(V.tensor_tensor(ge[:], keys.indirect(lst[:]), X, A.is_le))
-        return collect(ps, 20, [(T.FB, bp, True, [c_FB, eb]), (T.F, ge, True, [eg])])
+        return collect(ps, 20, [(T.FB, bp, True, [c_FB, ea, eb]), (T.F, ge, True, [eg])])
 
     def child(lst, e_lst, kg, ps):
         wait("s", e_lst)
@@ -304,10 +272,14 @@ def rank_program(g, core, T, topo):
     wait("v", a_x, r_sc, c_rt)
     w1 = ev(V.tensor_scalar(T.ge1[:], X, T.rootc[:, 0:1], None, A.is_ge))
     q1 = collect(T.p5, 20, [(T.F, T.ge1, True, [c_F, w1])])
+    wait("v", *e_nk)
+    d11 = ev(V.tensor_copy(T.nk2[:], T.nks[:].indirect(T.ml2[:, 0:1])))
     s2 = to_list(T.s2, T.p5, q1, -1)
     wait("v", d11)
     w2 = ev(V.tensor_tensor(T.ge2[:], T.nk2[:].indirect(T.s2[:]), X, A.is_le))
     q2 = collect(T.p6, 20, [(T.F16, T.ge1, True, [c_F16]), (T.F, T.ge2, True, [w2])])
+    wait("v", d12)
+    d13 = ev(V.tensor_copy(T.nk3[:], T.nks[:].indirect(T.ml3[:])))
     s3 = to_list(T.s3, T.p6, q2, -17)
     q3 = level(T.nk3[:], T.bl3[:], T.s3, s3, T.ge3, T.bp3, T.p4, [d13], [d14])
     e3 = to_list(T.e3, T.p4, q3, -1)
@@ -318,15 +290,16 @@ def rank_program(g, core, T, topo):
     vl = to_list(T.vl, T.p6, child(T.e5, e5, T.kg6, T.p6), 0)
 
     wait("v", e_vec)
-    va = ev(V.tensor_copy(T.ansb[:, 0:160], T.vecs[:].indirect(T.vl[:, 0:10])))
+    va = ev(V.tensor_copy(T.ansb[:, 0:128], T.vecs[:].indirect(T.vl[:, 0:8])))
     wait("s", e_vec, vl)
-    vb = ev(S.activation(T.ansb[:, 160:320], T.vecs[:].indirect(T.vl[:, 10:20]), AF.Copy))
+    vb = ev(S.activation(T.ansb[:, 128:256], T.vecs[:].indirect(T.vl[:, 8:16]), AF.Copy))
+    vc = ev(V.tensor_copy(T.ansb[:, 256:320], T.vecs[:].indirect(T.vl[:, 16:20])))
     wait("g", va, vb)
     send(T.ansb, lambda r: CAP * ((r - own) % N - 1), lambda r: 240 + CAP * ((own - r) % N), T.sem.arry, T.sem.lsy)
     a_y = ("arry", 12)
 
-    wait("v", a_y, vb, va, r_posg)
-    wait("s", a_y, va, vb, r_posg)
+    wait("v", a_y, va, vb, vc, r_posg)
+    wait("s", a_y, va, vb, vc, r_posg)
     y1 = ev(V.tensor_copy(T.yb[:, 0:128], T.ansb[:, 240:560].indirect(T.posG[:, 0:8])))
     y2 = ev(S.activation(T.yb[:, 128:256], T.ansb[:, 240:560].indirect(T.posG[:, 8:16]), AF.Copy))
     wait("y", y1, y2)

@@ -4,7 +4,7 @@ from concourse.mybir import AluOpType as A, ActivationFunctionType as AF
 CAP = 80
 NS = 4 * CAP
 FILL = 16777214
-HALF = 2048
+NKA, NKB = 1536, 2304
 
 SCRATCH = {
     "x": ("sbuf", [128, 256], "int32"),
@@ -24,18 +24,20 @@ SCRATCH = {
     "row": ("sbuf", [128, 144], "float32"),
     "qg": ("sbuf", [128, 128], "float32"),
     "sel": ("sbuf", [128, 128], "float32"),
-    "km": ("sbuf", [128, 16], "bfloat16"),
+    "Id16": ("sbuf", [128, 128], "float32"),
+    "s2f": ("sbuf", [128, 20], "float32"),
+    "m2b": ("sbuf", [128, 16], "bfloat16"),
     "bm": ("sbuf", [128, 16], "bfloat16"),
     "nk2": ("sbuf", [128, 16], "int32"),
     "nk3": ("sbuf", [128, 256], "int32"),
 }
-for _n in ("pid", "pidw", "wi", "oi", "gi", "spli"):
+for _n in ("pid", "oi", "gi", "spli"):
     SCRATCH[_n] = ("sbuf", [128, 8], "int32")
-for _n in ("w", "icol", "gcol", "g16", "m0", "m2c", "m4", "mB", "big", "thr", "rootc", "splf"):
+for _n in ("w", "wa", "wb", "pidf", "icol", "gcol", "g16", "m0", "m2c", "mB", "big", "thr", "rootc", "splf"):
     SCRATCH[_n] = ("sbuf", [128, 8], "float32")
-for _n in ("F", "F4", "FK", "FB", "F16"):
+for _n in ("F", "FW", "FK", "FB"):
     SCRATCH[_n] = ("sbuf", [128, 144], "bfloat16")
-for _n in ("Dm", "Ball", "BallB", "R0"):
+for _n in ("Dm", "Id", "Ball", "BallB", "R0", "km"):
     SCRATCH[_n] = ("sbuf", [128, 128], "bfloat16")
 for _n in ("geo", "H", "prod", "kg3", "bl3"):
     SCRATCH[_n] = ("sbuf", [128, 256], "bfloat16")
@@ -48,7 +50,7 @@ for _n in ("ge1", "ge2", "ge3", "ge4", "ge5", "kg4", "kg5", "kg6", "bp3", "bp4",
 for _n in range(8):
     SCRATCH["p%d" % _n] = ("psum", [128, 512], "float32")
 
-SEMAPHORES = ["arrx", "arry", "lsx", "lsy", "xl", "sent"] + ["e%d" % _k for _k in range(130)]
+SEMAPHORES = ["arrx", "arry", "lsx", "lsy", "xl", "sent"] + ["e%d" % _k for _k in range(144)]
 
 
 def rank_program(g, core, T, topo):
@@ -78,7 +80,7 @@ def rank_program(g, core, T, topo):
                         queue.wait_ge(T.sem[k], n)
                         done[q][k] = n
 
-    def collect(ps, n, terms):
+    def collect(ps, n, terms, first=True):
         tot = 16 * len(terms)
         k = 0
         last = None
@@ -86,7 +88,19 @@ def rank_program(g, core, T, topo):
             wait("p", *events)
             for i in range(16):
                 r = rhs[:, i:16 * n:16] if stepped else rhs[:, 16 * i:16 * i + n]
-                last = P.matmul(ps[:, 0:n], fb[:, 16 - i:144 - i], r, k == 0, k == tot - 1)
+                last = P.matmul(ps[:, 0:n], fb[:, 16 - i:144 - i], r, first and k == 0, k == tot - 1)
+                k += 1
+        return ev(last)
+
+    def halves(ps, terms):
+        tot = 8 * len(terms)
+        k = 0
+        last = None
+        for fb, rhs, h, events in terms:
+            wait("p", *events)
+            for i in range(8):
+                last = P.matmul(ps[:, 0:20], fb[:, 16 - 8 * h - i:144 - 8 * h - i], rhs[:, 160 * h + i:160 * h + 160:8],
+                                k == 0, k == tot - 1)
                 k += 1
         return ev(last)
 
@@ -96,90 +110,103 @@ def rank_program(g, core, T, topo):
         q = Y if o % 2 == 0 else S
         q.dma_start(T.x[o::16, :], T.q[:]).then_inc(T.sem.xl, 16)
     e_x = ("xl", 256)
-    e_kid = dm(Y.dma_start(T.kidc[:], T.kid[:]))
-    e_nk = [dm(Y.dma_start(T.nks[:, 0:HALF], T.nk[:, 0:HALF]))]
+    e_kid = dm(S.dma_start(T.kidc[:], T.kid[:]))
+    e_nk = [dm(Y.dma_start(T.nks[:, 0:NKA], T.nk[:, 0:NKA]))]
 
     z = ev(V.memset(T.Dm[:], 0.0))
     z2 = ev(V.memset(T.sel[0:32, :], 0.0))
-    f1 = ev(V.memset(T.TB[:, 0:1536], 0.0))
+    f1 = ev(V.memset(T.TB[:, 0:1792], 0.0))
     i_pid = ev(g.iota(T.pid[:, 0:1], [[1, 1]], 0, 1))
-    i_pw = ev(g.iota(T.pidw[:, 0:1], [[1, 1]], N - own, 1))
     i_row = ev(g.iota(T.row[:], [[1, 144]], 0, 0, allow_small_or_imprecise_dtypes=True))
     wait("g", z2)
     c_sel = ev(g.affine_select(T.sel[0:32, :], T.sel[0:32, :], [[-4, 8], [-1, 16]], A.not_equal, 1.0, 0, 1))
-    wait("g", z)
-    c_d1 = ev(g.affine_select(T.Dm[:], T.Dm[:], [[-1, 128]], A.not_equal, 1.0, 0, 1))
-    wait("g", c_d1)
-    c_D = ev(g.affine_select(T.Dm[:], T.Dm[:], [[-1, 128]], A.not_equal, -1.0, -1, 1))
-    fx = ev(g.iota(T.xq[:, 240:560], [[0, 320]], FILL, 0))
+    c_D = z
+    for step, fill, base in (([[-1, 128]], 2.0, 0), ([[-1, 128]], -1.0, -1), ([[-1, 128]], -1.0, 1),
+                             ([[-16, 8], [-1000, 16]], 1.0, 0)):
+        wait("g", c_D)
+        c_D = ev(g.affine_select(T.Dm[:], T.Dm[:], step, A.not_equal, fill, base, 1))
     i_qg = ev(g.iota(T.qg[:], [[1, 8], [0, 16]], 0, 0, allow_small_or_imprecise_dtypes=True))
-    f4 = ev(g.iota(T.TB[:, 5632:6144], [[0, 512]], 0, 0, allow_small_or_imprecise_dtypes=True))
+    fx = ev(g.iota(T.xq[:, 240:560], [[0, 320]], FILL, 0))
+    f4 = ev(g.iota(T.TB[:, 5760:6144], [[0, 384]], 0, 0, allow_small_or_imprecise_dtypes=True))
 
     zs = ev(V.memset(T.Z[:], 0.0))
-    wait("v", i_pid, i_pw)
+    wait("v", i_pid)
     c_o = ev(V.tensor_scalar(T.oi[:, 0:1], T.pid[:, 0:1], 15, None, A.bitwise_and))
     c_g = ev(V.tensor_scalar(T.gi[:, 0:1], T.pid[:, 0:1], 4, None, A.arith_shift_right))
-    c_wi = ev(V.tensor_scalar(T.wi[:, 0:1], T.pidw[:, 0:1], 3, None, A.bitwise_and))
-    wait("v", c_o, c_g, c_wi)
+    c_pf = ev(V.tensor_copy(T.pidf[:, 0:1], T.pid[:, 0:1]))
+    f3 = ev(V.memset(T.TB[:, 5376:5760], 0.0))
+    wait("v", c_o, c_g)
     c_g16 = ev(V.tensor_scalar(T.g16[:, 0:1], T.gi[:, 0:1], 16.0, 16.0, A.mult, A.add))
-    c_m4 = ev(V.tensor_scalar(T.m4[:, 0:1], T.oi[:, 0:1], 4.0, None, A.is_lt))
     c_big = ev(V.tensor_scalar(T.big[:, 0:1], T.oi[:, 0:1], 4.0, 33554432.0, A.is_ge, A.mult))
-    c_w = ev(V.tensor_scalar(T.w[:, 0:1], T.wi[:, 0:1], 80.0, -161.0, A.mult, A.add))
-    wait("v", c_g16, i_row)
+    c_wa = ev(V.tensor_scalar(T.wa[:, 0:1], T.oi[:, 0:1], float(own), -4.0 * CAP, A.is_equal, A.mult))
+    c_wb = ev(V.tensor_scalar(T.wb[:, 0:1], T.oi[:, 0:1], 0.0, float(CAP * (N - 1 - own)), A.is_equal, A.mult))
+    wait("v", c_pf, i_row)
+    c_Id = ev(V.tensor_scalar(T.Id[:], T.row[:, 0:128], T.pidf[:, 0:1], None, A.is_equal))
+    wait("v", c_g16)
     c_F = ev(V.tensor_scalar(T.F[:], T.row[:], T.g16[:, 0:1], None, A.is_equal))
+    wait("v", c_wa, c_wb)
+    c_w = ev(V.tensor_scalar(T.w[:, 0:1], T.wa[:, 0:1], float(CAP), T.wb[:, 0:1], A.add, A.add))
     wait("v", e_spl)
     c_sf = ev(V.tensor_copy(T.splf[0:32, 0:1], T.spli[0:32, 0:1]))
     wait("p", c_sf, c_sel)
     p_thr = ev(P.matmul(T.p0[:, 0:1], T.sel[0:32, :], T.splf[0:32, 0:1], True, True))
-    wait("v", p_thr, c_big)
-    c_thr = ev(V.tensor_scalar(T.thr[:, 0:1], T.p0[:, 0:1], T.big[:, 0:1], None, A.add))
     wait("v", e_beg)
     b_hi = ev(V.tensor_copy(T.bhi[:], T.begc[:]))
-    wait("v", b_hi)
-    b_lo = ev(V.tensor_tensor(T.blo[:], T.begc[:], T.bhi[:], A.subtract))
+    wait("p", c_Id, b_hi)
+    b_ps = ev(P.matmul(T.p6[:, 0:192], T.Id[:], T.bhi[:], True, True))
+    wait("v", c_F, c_w)
+    c_FW = ev(V.tensor_scalar(T.FW[:], T.F[:], T.w[:, 0:1], None, A.mult))
+    wait("v", p_thr, c_big)
+    c_thr = ev(V.tensor_scalar(T.thr[:, 0:1], T.p0[:, 0:1], T.big[:, 0:1], None, A.add))
+    wait("v", b_ps)
+    b_lo = ev(V.tensor_tensor(T.blo[:], T.begc[:], T.p6[:, 0:192], A.subtract))
 
     wait("s", f1)
-    f2 = [ev(S.activation(T.TB[:, 1536:3072], T.TB[:, 0:1536], AF.Copy))]
-    wait("s", c_F, c_m4)
-    c_F4 = ev(S.activation(T.F4[:], T.F[:], AF.Identity, scale=T.m4[:, 0:1]))
-    f2.append(ev(S.activation(T.TB[:, 3072:4608], T.TB[:, 0:1536], AF.Copy)))
-    f2.append(ev(S.activation(T.TB[:, 4608:5632], T.TB[:, 0:1024], AF.Copy)))
+    f2 = [ev(S.activation(T.TB[:, 1792:3584], T.TB[:, 0:1792], AF.Copy))]
+    f2.append(ev(S.activation(T.TB[:, 3584:5376], T.TB[:, 0:1792], AF.Copy)))
 
     wait("v", e_x, c_thr)
     r_ge = ev(V.tensor_scalar(T.geo[:], T.x[:], T.thr[:, 0:1], None, A.is_ge))
-    wait("p", c_D, r_ge)
-    r_oh = ev(P.matmul(T.p1[:, 0:256], T.Dm[:], T.geo[:], True, True))
+    wait("v", zs, r_ge)
+    r_h = ev(V.tensor_tensor_scan(T.H[:], T.geo[:], T.Z[:], 0.0, A.add, A.add))
+    wait("p", c_FW, r_ge)
+    for i in range(4):
+        P.matmul(T.p2[:, 0:16], T.FW[:, 16 - i:144 - i], T.geo[:, i:256:16], i == 0, False)
+    wait("p", c_D, r_h)
+    r_oh = ev(P.matmul(T.p1[:, 0:256], T.Dm[:], T.H[:], True, True))
     wait("v", e_kid)
     k_hi = ev(V.tensor_copy(T.khi[:], T.kidc[:]))
-    wait("v", r_oh, zs, c_w)
-    r_h = ev(V.tensor_tensor_scan(T.H[:], T.p1[:, 0:256], T.Z[:], T.w[:, 0:1], A.add, A.add))
-    wait("v", r_h)
-    r_pr = ev(V.tensor_tensor(T.prod[:], T.H[:], T.p1[:, 0:256], A.mult))
-    r_ps = collect(T.p2, 16, [(T.F4, T.prod, True, [c_F4, r_pr])])
-    r_pg = collect(T.p3, 16, [(T.F4, T.prod, False, [])])
-    wait("v", k_hi)
-    k_lo = ev(V.tensor_tensor(T.klo[:], T.kidc[:], T.khi[:], A.subtract))
+    wait("v", r_oh)
+    r_pr = ev(V.tensor_tensor(T.prod[:], T.p1[:, 0:256], T.geo[:], A.mult))
+    for i in range(4, 16):
+        P.matmul(T.p2[:, 0:16], T.FW[:, 16 - i:144 - i], T.geo[:, i:256:16], False, False)
+    wait("p", k_hi)
+    k_ps = ev(P.matmul(T.p7[:, 0:384], T.Id[:], T.khi[:], True, True))
+    r_ps = collect(T.p2, 16, [(T.F, T.prod, True, [c_F, r_pr])], False)
+    r_pg = collect(T.p3, 16, [(T.FW, T.geo, False, []), (T.F, T.prod, False, [])])
+    c_gc = ev(V.tensor_copy(T.gcol[:, 0:1], T.gi[:, 0:1]))
+    c_m0 = ev(V.tensor_scalar(T.m0[:, 0:1], T.oi[:, 0:1], 0.0, None, A.is_equal))
+    c_i = ev(V.tensor_copy(T.icol[:, 0:1], T.oi[:, 0:1]))
+    wait("v", k_ps)
+    k_lo = ev(V.tensor_tensor(T.klo[:], T.kidc[:], T.p7[:, 0:384], A.subtract))
+    wait("v", i_qg, c_gc)
+    c_B = ev(V.tensor_scalar(T.Ball[:], T.qg[:], T.gcol[:, 0:1], None, A.is_equal))
     wait("v", r_ps)
-    r_pos = ev(V.tensor_scalar(T.posS[:], T.p2[:, 0:16], 160.0, None, A.add))
+    r_pos = ev(V.tensor_scalar(T.posS[:], T.p2[:, 0:16], -1.0, None, A.add))
     wait("v", r_pos, fx)
     r_sc = ev(V.tensor_copy(T.xq[:, 240:560].indirect(T.posS[:, 0:16]), T.x[:]))
 
-    wait("v", i_qg)
-    c_i = ev(V.tensor_copy(T.icol[:, 0:1], T.oi[:, 0:1]))
-    c_gc = ev(V.tensor_copy(T.gcol[:, 0:1], T.gi[:, 0:1]))
     c_m2 = ev(V.tensor_scalar(T.m2c[:, 0:1], T.oi[:, 0:1], 2.0, None, A.is_lt))
-    c_m0 = ev(V.tensor_scalar(T.m0[:, 0:1], T.oi[:, 0:1], 0.0, None, A.is_equal))
-    wait("v", c_gc, c_m4, c_m2, c_i)
-    c_B = ev(V.tensor_scalar(T.Ball[:], T.qg[:], T.gcol[:, 0:1], None, A.is_equal))
-    c_mB = ev(V.tensor_tensor(T.mB[:, 0:1], T.m4[:, 0:1], T.m2c[:, 0:1], A.subtract))
+    c_mB = ev(V.tensor_scalar(T.mB[:, 0:1], T.oi[:, 0:1], 14.0, None, A.is_ge))
     wait("s", c_B, c_m0)
     c_R0 = ev(S.activation(T.R0[:], T.Ball[:], AF.Identity, scale=T.m0[:, 0:1]))
     wait("s", c_m2)
-    c_FK = ev(S.activation(T.FK[:], T.F[:], AF.Identity, scale=T.m2c[:, 0:1]))
+    c_mb = ev(S.activation(T.m2b[:, 0:1], T.m2c[:, 0:1], AF.Copy))
     wait("s", c_mB)
     c_BB = ev(S.activation(T.BallB[:], T.Ball[:], AF.Identity, scale=T.mB[:, 0:1]))
-    c_F16 = ev(S.activation(T.F16[:], T.F[:], AF.Copy, scale=16.0))
+    c_FK = ev(S.activation(T.FK[:], T.F[:], AF.Identity, scale=T.m2c[:, 0:1]))
     c_FB = ev(S.activation(T.FB[:], T.F[:], AF.Identity, scale=T.mB[:, 0:1]))
+    c_I16 = ev(S.activation(T.Id16[:], T.Id[:], AF.Copy, scale=16.0))
 
     near = [r for r in range(N) if r != own and topo.die(T.cores[r]) == topo.die(core)]
     far = [r for r in range(N) if r != own and topo.die(T.cores[r]) != topo.die(core)]
@@ -203,96 +230,113 @@ def rank_program(g, core, T, topo):
     a_x = ("arrx", 12)
     g.sem_inc(T.sem.sent, 1)
 
-    wait("y", b_hi, b_lo, f1, f4, *f2)
-    t_b = dm(Y.dma_start(T.TB[2::16, 0:3072], T.bhi[:]))
-    t_c = dm(Y.dma_start(T.TB[3::16, 0:3072], T.blo[:]))
+    wait("y", b_hi, b_lo, f1, f3, f4, *f2)
+    t_b = dm(Y.dma_start(T.TB[14::16, 0:3072], T.bhi[:]))
+    t_c = dm(Y.dma_start(T.TB[15::16, 0:3072], T.blo[:]))
     wait("y", k_hi, k_lo)
     t_k = dm(Y.dma_start(T.TB[0::16, :], T.khi[:]))
     t_l = dm(Y.dma_start(T.TB[1::16, :], T.klo[:]))
+    e_nk.append(dm(Y.dma_start(T.nks[:, NKA:NKB], T.nk[:, NKA:NKB])))
     wait("y", ("sent", 1))
-    e_nk.append(dm(Y.dma_start(T.nks[:, HALF:3072], T.nk[:, HALF:3072])))
+    e_nk.append(dm(Y.dma_start(T.nks[:, NKB:3072], T.nk[:, NKB:3072])))
     e_vec = dm(Y.dma_start(T.vecs[:], T.vec[:]))
     tb = [t_k, t_l, t_b, t_c]
-
-    wait("v", r_pg)
-    r_posg = ev(V.tensor_scalar(T.posG[:], T.p3[:, 0:16], 160.0, None, A.add))
 
     X = T.xq[:, 0:NS]
     wait("p", c_R0, b_hi, b_lo)
     P.matmul(T.p4[:, 0:1], T.R0[:], T.bhi[:, 0:1], True, False)
     d0 = ev(P.matmul(T.p4[:, 0:1], T.R0[:], T.blo[:, 0:1], False, True))
-    wait("v", d0)
-    d1 = ev(V.tensor_scalar(T.e1[:, 0:1], T.p4[:, 0:1], T.icol[:, 0:1], None, A.add))
+    wait("v", d0, c_i)
+    d1 = ev(V.tensor_scalar(T.e1[:, 0:8], T.Z[:, 0:8], T.p4[:, 0:1], T.icol[:, 0:1], A.add, A.add))
     wait("v", d1, *tb)
-    d2 = ev(V.tensor_copy(T.km[:], T.TB[:].indirect(T.e1[:, 0:1])))
-    d3 = collect(T.p5, 1, [(T.FK, T.km, True, [c_FK, d2])])
+    d2 = ev(V.tensor_tensor(T.km[:], T.TB[:].indirect(T.e1[:, 0:8]), T.Ball[:], A.mult))
+    wait("p", c_mb, d2)
+    d3 = ev(P.matmul(T.p5[:, 0:1], T.km[:], T.m2b[:, 0:1], True, True))
     wait("v", d3)
     d4 = ev(V.tensor_copy(T.ml2[:, 0:1], T.p5[:, 0:1]))
     wait("v", d4)
     d5 = ev(V.tensor_copy(T.bm[:], T.TB[:, 0:3072].indirect(T.ml2[:, 0:1])))
     wait("p", c_BB, d5)
     d6 = ev(P.matmul(T.p6[:, 0:16], T.BallB[:], T.bm[:], True, True))
+    wait("v", r_pg)
+    r_posg = ev(V.tensor_scalar(T.posG[:], T.p3[:, 0:16], -1.0, None, A.add))
+    wait("v", e_nk[0])
+    c_rt = ev(V.tensor_copy(T.rootc[:, 0:1], T.nks[:, 0:1]))
+
+    def to_list(buf, ps, event, add):
+        wait("v", event)
+        e = ev(V.tensor_scalar(buf[:], ps[:, 0:20], float(add), None, A.add))
+        wait("v", e)
+        return e
+
+    def two_lists(buf, ps, event, add):
+        wait("v", event)
+        return [ev(V.tensor_scalar(buf[:, 10 * p:10 * p + 10], ps[:, p:20:2], float(add), None, A.add)) for p in range(2)]
+
+    def level(keys, starts, lst, el, ge, bp, ps, deps_v, deps_s):
+        wait("s", el[0], *deps_s)
+        ea = ev(S.activation(bp[:, 64:160], starts.indirect(lst[:, 4:10]), AF.Copy))
+        wait("v", el[0], *deps_v, *deps_s)
+        eb = ev(V.tensor_copy(bp[:, 0:64], starts.indirect(lst[:, 0:4])))
+        g0 = ev(V.tensor_tensor(ge[:, 0:160], keys.indirect(lst[:, 0:10]), T.xq[:, 0:160], A.is_le))
+        wait("s", el[1])
+        ec = ev(S.activation(bp[:, 160:320], starts.indirect(lst[:, 10:20]), AF.Copy))
+        wait("v", el[1])
+        g1 = ev(V.tensor_tensor(ge[:, 160:320], keys.indirect(lst[:, 10:20]), T.xq[:, 160:320], A.is_le))
+        return halves(ps, [(T.FB, bp, 0, [c_FB, ea, eb]), (T.F, ge, 0, [g0]), (T.FB, bp, 1, [ec]), (T.F, ge, 1, [g1])])
+
+    def child(lst, el, kg, ps):
+        ee = []
+        for h, va in enumerate((6, 4)):
+            c = 10 * h
+            wait("s", el[h])
+            a = ev(S.activation(kg[:, 16 * (c + va):16 * (c + 10)], T.TB[:].indirect(lst[:, c + va:c + 10]), AF.Copy))
+            wait("v", el[h])
+            b = ev(V.tensor_copy(kg[:, 16 * c:16 * (c + va)], T.TB[:].indirect(lst[:, c:c + va])))
+            ee.append([a, b])
+        return halves(ps, [(T.FK, kg, 0, [c_FK] + ee[0]), (T.FK, kg, 1, ee[1])])
+
+    wait("v", r_sc, c_rt)
+    w0 = ev(V.tensor_scalar(T.ge1[:, 240:320], T.xq[:, 240:320], T.rootc[:, 0:1], None, A.is_ge))
+    wait("v", a_x)
+    w1 = ev(V.tensor_scalar(T.ge1[:, 0:240], T.xq[:, 0:240], T.rootc[:, 0:1], None, A.is_ge))
+    q1 = collect(T.p5, 20, [(T.F, T.ge1, True, [c_F, w0, w1])])
     wait("v", d6)
     d7 = ev(V.tensor_scalar(T.e2[:], T.p6[:, 0:16], T.icol[:, 0:1], None, A.add))
     wait("v", d7)
     d8 = ev(V.tensor_copy(T.kg3[:, 0:128], T.TB[:].indirect(T.e2[:, 0:8])))
     wait("s", d7, *tb)
     d9 = ev(S.activation(T.kg3[:, 128:256], T.TB[:].indirect(T.e2[:, 8:16]), AF.Copy))
-    d10 = collect(T.p4, 16, [(T.FK, T.kg3, True, [d8, d9])])
-    wait("v", e_nk[0])
-    c_rt = ev(V.tensor_copy(T.rootc[:, 0:1], T.nks[:, 0:1]))
+    d10 = collect(T.p4, 16, [(T.FK, T.kg3, True, [c_FK, d8, d9])])
+    wait("v", *e_nk)
+    d11 = ev(V.tensor_copy(T.nk2[:], T.nks[:].indirect(T.ml2[:, 0:1])))
+    s2 = to_list(T.s2, T.p5, q1, -1)
+    wait("s", s2)
+    s2f = ev(S.activation(T.s2f[:], T.p5[:, 0:20], AF.Copy))
+    wait("v", d11)
+    w2 = ev(V.tensor_tensor(T.ge2[:], T.nk2[:].indirect(T.s2[:]), X, A.is_le))
+    wait("p", s2f, c_I16)
+    P.matmul(T.p6[:, 0:20], T.Id16[:], T.s2f[:], True, False)
+    q2 = collect(T.p6, 20, [(T.F, T.ge2, True, [w2])], False)
     wait("v", d10)
     d12 = ev(V.tensor_copy(T.ml3[:], T.p4[:, 0:16]))
     wait("s", d12)
     d14 = ev(S.activation(T.bl3[:], T.TB[:, 0:3072].indirect(T.ml3[:]), AF.Copy))
-
-    def to_list(buf, ps, event, add):
-        wait("v", event)
-        if add:
-            e = ev(V.tensor_scalar(buf[:], ps[:, 0:20], float(add), None, A.add))
-        else:
-            e = ev(V.tensor_copy(buf[:], ps[:, 0:20]))
-        wait("v", e)
-        return e
-
-    def level(keys, starts, lst, e_lst, ge, bp, ps, deps_v, deps_s):
-        wait("s", e_lst, *deps_s)
-        ea = ev(S.activation(bp[:, 0:192], starts.indirect(lst[:, 0:12]), AF.Copy))
-        wait("v", *deps_v, *deps_s)
-        eb = ev(V.tensor_copy(bp[:, 192:320], starts.indirect(lst[:, 12:20])))
-        eg = ev(V.tensor_tensor(ge[:], keys.indirect(lst[:]), X, A.is_le))
-        return collect(ps, 20, [(T.FB, bp, True, [c_FB, ea, eb]), (T.F, ge, True, [eg])])
-
-    def child(lst, e_lst, kg, ps):
-        wait("s", e_lst)
-        a = ev(S.activation(kg[:, 160:320], T.TB[:].indirect(lst[:, 10:20]), AF.Copy))
-        b = ev(V.tensor_copy(kg[:, 0:160], T.TB[:].indirect(lst[:, 0:10])))
-        return collect(ps, 20, [(T.FK, kg, True, [a, b])])
-
-    wait("v", a_x, r_sc, c_rt)
-    w1 = ev(V.tensor_scalar(T.ge1[:], X, T.rootc[:, 0:1], None, A.is_ge))
-    q1 = collect(T.p5, 20, [(T.F, T.ge1, True, [c_F, w1])])
-    wait("v", *e_nk)
-    d11 = ev(V.tensor_copy(T.nk2[:], T.nks[:].indirect(T.ml2[:, 0:1])))
-    s2 = to_list(T.s2, T.p5, q1, -1)
-    wait("v", d11)
-    w2 = ev(V.tensor_tensor(T.ge2[:], T.nk2[:].indirect(T.s2[:]), X, A.is_le))
-    q2 = collect(T.p6, 20, [(T.F16, T.ge1, True, [c_F16]), (T.F, T.ge2, True, [w2])])
     wait("v", d12)
     d13 = ev(V.tensor_copy(T.nk3[:], T.nks[:].indirect(T.ml3[:])))
     s3 = to_list(T.s3, T.p6, q2, -17)
-    q3 = level(T.nk3[:], T.bl3[:], T.s3, s3, T.ge3, T.bp3, T.p4, [d13], [d14])
-    e3 = to_list(T.e3, T.p4, q3, -1)
-    n4 = to_list(T.n4, T.p5, child(T.e3, e3, T.kg4, T.p5), 0)
-    e4 = to_list(T.e4, T.p6, level(T.nks[:], T.TB[:, 0:3072], T.n4, n4, T.ge4, T.bp4, T.p6, [], []), -1)
-    n5 = to_list(T.n5, T.p4, child(T.e4, e4, T.kg5, T.p4), 0)
-    e5 = to_list(T.e5, T.p5, level(T.nks[:], T.TB[:, 0:3072], T.n5, n5, T.ge5, T.bp5, T.p5, [], []), -1)
-    vl = to_list(T.vl, T.p6, child(T.e5, e5, T.kg6, T.p6), 0)
+    e3 = two_lists(T.e3, T.p4, level(T.nk3[:], T.bl3[:], T.s3, [s3, s3], T.ge3, T.bp3, T.p4, [d13], [d14]), -1)
+    n4 = two_lists(T.n4, T.p5, child(T.e3, e3, T.kg4, T.p5), 0)
+    e4 = two_lists(T.e4, T.p6, level(T.nks[:], T.TB[:, 0:3072], T.n4, n4, T.ge4, T.bp4, T.p6, [], []), -1)
+    n5 = two_lists(T.n5, T.p4, child(T.e4, e4, T.kg5, T.p4), 0)
+    e5 = two_lists(T.e5, T.p5, level(T.nks[:], T.TB[:, 0:3072], T.n5, n5, T.ge5, T.bp5, T.p5, [], []), -1)
+    vl = two_lists(T.vl, T.p6, child(T.e5, e5, T.kg6, T.p6), 0)
 
-    wait("v", e_vec)
+    wait("v", e_vec, vl[0])
     va = ev(V.tensor_copy(T.ansb[:, 0:128], T.vecs[:].indirect(T.vl[:, 0:8])))
-    wait("s", e_vec, vl)
+    wait("s", e_vec, *vl)
     vb = ev(S.activation(T.ansb[:, 128:256], T.vecs[:].indirect(T.vl[:, 8:16]), AF.Copy))
+    wait("v", vl[1])
     vc = ev(V.tensor_copy(T.ansb[:, 256:320], T.vecs[:].indirect(T.vl[:, 16:20])))
     wait("g", va, vb)
     send(T.ansb, lambda r: CAP * ((r - own) % N - 1), lambda r: 240 + CAP * ((own - r) % N), T.sem.arry, T.sem.lsy)

from concourse.bass import DstId, RemoteDMATransfer
from concourse.mybir import AluOpType as A, ActivationFunctionType as AF

CAP = 80
NS = 4 * CAP
FILL = 16777214
NKA, NKB = 1536, 2304

SCRATCH = {
    "x": ("sbuf", [128, 256], "int32"),
    "xq": ("sbuf", [128, 560], "int32"),
    "ansb": ("sbuf", [128, 560], "bfloat16"),
    "yb": ("sbuf", [128, 256], "bfloat16"),
    "nks": ("sbuf", [128, 3072], "int32"),
    "vecs": ("sbuf", [128, 3072], "bfloat16"),
    "TB": ("sbuf", [128, 6144], "bfloat16"),
    "kidc": ("sbuf", [128, 384], "int32"),
    "begc": ("sbuf", [128, 192], "int32"),
    "khi": ("sbuf", [128, 384], "bfloat16"),
    "klo": ("sbuf", [128, 384], "bfloat16"),
    "bhi": ("sbuf", [128, 192], "bfloat16"),
    "blo": ("sbuf", [128, 192], "bfloat16"),
    "Z": ("sbuf", [128, 256], "bfloat16"),
    "row": ("sbuf", [128, 144], "float32"),
    "qg": ("sbuf", [128, 128], "float32"),
    "sel": ("sbuf", [128, 128], "float32"),
    "Id16": ("sbuf", [128, 128], "float32"),
    "s2f": ("sbuf", [128, 20], "float32"),
    "m2b": ("sbuf", [128, 16], "bfloat16"),
    "bm": ("sbuf", [128, 16], "bfloat16"),
    "nk2": ("sbuf", [128, 16], "int32"),
    "nk3": ("sbuf", [128, 256], "int32"),
}
for _n in ("pid", "oi", "gi", "spli"):
    SCRATCH[_n] = ("sbuf", [128, 8], "int32")
for _n in ("w", "wa", "wb", "pidf", "icol", "gcol", "g16", "m0", "m2c", "mB", "big", "thr", "rootc", "splf"):
    SCRATCH[_n] = ("sbuf", [128, 8], "float32")
for _n in ("F", "FW", "FK", "FB"):
    SCRATCH[_n] = ("sbuf", [128, 144], "bfloat16")
for _n in ("Dm", "Id", "Ball", "BallB", "R0", "km"):
    SCRATCH[_n] = ("sbuf", [128, 128], "bfloat16")
for _n in ("geo", "H", "prod", "kg3", "bl3"):
    SCRATCH[_n] = ("sbuf", [128, 256], "bfloat16")
for _n in ("posS", "posG", "e1", "ml2", "e2", "ml3"):
    SCRATCH[_n] = ("sbuf", [128, 16], "uint16")
for _n in ("s2", "s3", "e3", "n4", "e4", "n5", "e5", "vl"):
    SCRATCH[_n] = ("sbuf", [128, 20], "uint16")
for _n in ("ge1", "ge2", "ge3", "ge4", "ge5", "kg4", "kg5", "kg6", "bp3", "bp4", "bp5"):
    SCRATCH[_n] = ("sbuf", [128, NS], "bfloat16")
for _n in range(8):
    SCRATCH["p%d" % _n] = ("psum", [128, 512], "float32")

SEMAPHORES = ["arrx", "arry", "lsx", "lsy", "xl", "sent"] + ["e%d" % _k for _k in range(144)]


def rank_program(g, core, T, topo):
    own = T.rank_of(core)
    if own is None:
        return
    N = 4
    V, S, P, Y = g.vector, g.scalar, g.tensor, g.sync
    used = [0]
    done = {"v": {}, "s": {}, "p": {}, "y": {}, "g": {}}
    names = (("v", V), ("s", S), ("p", P), ("y", Y), ("g", g))

    def ev(inst, n=1):
        k = "e%d" % used[0]
        used[0] += 1
        inst.then_inc(T.sem[k], n)
        return (k, n)

    def dm(inst):
        return ev(inst, 16)

    def wait(q, *events):
        for name, queue in names:
            if name == q:
                for k, n in events:
                    if done[q].get(k, 0) < n:
                        queue.wait_ge(T.sem[k], n)
                        done[q][k] = n

    def collect(ps, n, terms, first=True):
        tot = 16 * len(terms)
        k = 0
        last = None
        for fb, rhs, stepped, events in terms:
            wait("p", *events)
            for i in range(16):
                r = rhs[:, i:16 * n:16] if stepped else rhs[:, 16 * i:16 * i + n]
                last = P.matmul(ps[:, 0:n], fb[:, 16 - i:144 - i], r, first and k == 0, k == tot - 1)
                k += 1
        return ev(last)

    def halves(ps, terms):
        tot = 8 * len(terms)
        k = 0
        last = None
        for fb, rhs, h, events in terms:
            wait("p", *events)
            for i in range(8):
                last = P.matmul(ps[:, 0:20], fb[:, 16 - 8 * h - i:144 - 8 * h - i], rhs[:, 160 * h + i:160 * h + 160:8],
                                k == 0, k == tot - 1)
                k += 1
        return ev(last)

    e_beg = dm(S.dma_start(T.begc[:], T.beg[:]))
    e_spl = dm(Y.dma_start(T.spli[0:32, 0:1], T.spl[:]))
    for o in range(16):
        q = Y if o % 2 == 0 else S
        q.dma_start(T.x[o::16, :], T.q[:]).then_inc(T.sem.xl, 16)
    e_x = ("xl", 256)
    e_kid = dm(S.dma_start(T.kidc[:], T.kid[:]))
    e_nk = [dm(Y.dma_start(T.nks[:, 0:NKA], T.nk[:, 0:NKA]))]

    z = ev(V.memset(T.Dm[:], 0.0))
    z2 = ev(V.memset(T.sel[0:32, :], 0.0))
    f1 = ev(V.memset(T.TB[:, 0:1792], 0.0))
    i_pid = ev(g.iota(T.pid[:, 0:1], [[1, 1]], 0, 1))
    i_row = ev(g.iota(T.row[:], [[1, 144]], 0, 0, allow_small_or_imprecise_dtypes=True))
    wait("g", z2)
    c_sel = ev(g.affine_select(T.sel[0:32, :], T.sel[0:32, :], [[-4, 8], [-1, 16]], A.not_equal, 1.0, 0, 1))
    c_D = z
    for step, fill, base in (([[-1, 128]], 2.0, 0), ([[-1, 128]], -1.0, -1), ([[-1, 128]], -1.0, 1),
                             ([[-16, 8], [-1000, 16]], 1.0, 0)):
        wait("g", c_D)
        c_D = ev(g.affine_select(T.Dm[:], T.Dm[:], step, A.not_equal, fill, base, 1))
    i_qg = ev(g.iota(T.qg[:], [[1, 8], [0, 16]], 0, 0, allow_small_or_imprecise_dtypes=True))
    fx = ev(g.iota(T.xq[:, 240:560], [[0, 320]], FILL, 0))
    f4 = ev(g.iota(T.TB[:, 5760:6144], [[0, 384]], 0, 0, allow_small_or_imprecise_dtypes=True))

    zs = ev(V.memset(T.Z[:], 0.0))
    wait("v", i_pid)
    c_o = ev(V.tensor_scalar(T.oi[:, 0:1], T.pid[:, 0:1], 15, None, A.bitwise_and))
    c_g = ev(V.tensor_scalar(T.gi[:, 0:1], T.pid[:, 0:1], 4, None, A.arith_shift_right))
    c_pf = ev(V.tensor_copy(T.pidf[:, 0:1], T.pid[:, 0:1]))
    f3 = ev(V.memset(T.TB[:, 5376:5760], 0.0))
    wait("v", c_o, c_g)
    c_g16 = ev(V.tensor_scalar(T.g16[:, 0:1], T.gi[:, 0:1], 16.0, 16.0, A.mult, A.add))
    c_big = ev(V.tensor_scalar(T.big[:, 0:1], T.oi[:, 0:1], 4.0, 33554432.0, A.is_ge, A.mult))
    c_wa = ev(V.tensor_scalar(T.wa[:, 0:1], T.oi[:, 0:1], float(own), -4.0 * CAP, A.is_equal, A.mult))
    c_wb = ev(V.tensor_scalar(T.wb[:, 0:1], T.oi[:, 0:1], 0.0, float(CAP * (N - 1 - own)), A.is_equal, A.mult))
    wait("v", c_pf, i_row)
    c_Id = ev(V.tensor_scalar(T.Id[:], T.row[:, 0:128], T.pidf[:, 0:1], None, A.is_equal))
    wait("v", c_g16)
    c_F = ev(V.tensor_scalar(T.F[:], T.row[:], T.g16[:, 0:1], None, A.is_equal))
    wait("v", c_wa, c_wb)
    c_w = ev(V.tensor_scalar(T.w[:, 0:1], T.wa[:, 0:1], float(CAP), T.wb[:, 0:1], A.add, A.add))
    wait("v", e_spl)
    c_sf = ev(V.tensor_copy(T.splf[0:32, 0:1], T.spli[0:32, 0:1]))
    wait("p", c_sf, c_sel)
    p_thr = ev(P.matmul(T.p0[:, 0:1], T.sel[0:32, :], T.splf[0:32, 0:1], True, True))
    wait("v", e_beg)
    b_hi = ev(V.tensor_copy(T.bhi[:], T.begc[:]))
    wait("p", c_Id, b_hi)
    b_ps = ev(P.matmul(T.p6[:, 0:192], T.Id[:], T.bhi[:], True, True))
    wait("v", c_F, c_w)
    c_FW = ev(V.tensor_scalar(T.FW[:], T.F[:], T.w[:, 0:1], None, A.mult))
    wait("v", p_thr, c_big)
    c_thr = ev(V.tensor_scalar(T.thr[:, 0:1], T.p0[:, 0:1], T.big[:, 0:1], None, A.add))
    wait("v", b_ps)
    b_lo = ev(V.tensor_tensor(T.blo[:], T.begc[:], T.p6[:, 0:192], A.subtract))

    wait("s", f1)
    f2 = [ev(S.activation(T.TB[:, 1792:3584], T.TB[:, 0:1792], AF.Copy))]
    f2.append(ev(S.activation(T.TB[:, 3584:5376], T.TB[:, 0:1792], AF.Copy)))

    wait("v", e_x, c_thr)
    r_ge = ev(V.tensor_scalar(T.geo[:], T.x[:], T.thr[:, 0:1], None, A.is_ge))
    wait("v", zs, r_ge)
    r_h = ev(V.tensor_tensor_scan(T.H[:], T.geo[:], T.Z[:], 0.0, A.add, A.add))
    wait("p", c_FW, r_ge)
    for i in range(4):
        P.matmul(T.p2[:, 0:16], T.FW[:, 16 - i:144 - i], T.geo[:, i:256:16], i == 0, False)
    wait("p", c_D, r_h)
    r_oh = ev(P.matmul(T.p1[:, 0:256], T.Dm[:], T.H[:], True, True))
    wait("v", e_kid)
    k_hi = ev(V.tensor_copy(T.khi[:], T.kidc[:]))
    wait("v", r_oh)
    r_pr = ev(V.tensor_tensor(T.prod[:], T.p1[:, 0:256], T.geo[:], A.mult))
    for i in range(4, 16):
        P.matmul(T.p2[:, 0:16], T.FW[:, 16 - i:144 - i], T.geo[:, i:256:16], False, False)
    wait("p", k_hi)
    k_ps = ev(P.matmul(T.p7[:, 0:384], T.Id[:], T.khi[:], True, True))
    r_ps = collect(T.p2, 16, [(T.F, T.prod, True, [c_F, r_pr])], False)
    r_pg = collect(T.p3, 16, [(T.FW, T.geo, False, []), (T.F, T.prod, False, [])])
    c_gc = ev(V.tensor_copy(T.gcol[:, 0:1], T.gi[:, 0:1]))
    c_m0 = ev(V.tensor_scalar(T.m0[:, 0:1], T.oi[:, 0:1], 0.0, None, A.is_equal))
    c_i = ev(V.tensor_copy(T.icol[:, 0:1], T.oi[:, 0:1]))
    wait("v", k_ps)
    k_lo = ev(V.tensor_tensor(T.klo[:], T.kidc[:], T.p7[:, 0:384], A.subtract))
    wait("v", i_qg, c_gc)
    c_B = ev(V.tensor_scalar(T.Ball[:], T.qg[:], T.gcol[:, 0:1], None, A.is_equal))
    wait("v", r_ps)
    r_pos = ev(V.tensor_scalar(T.posS[:], T.p2[:, 0:16], -1.0, None, A.add))
    wait("v", r_pos, fx)
    r_sc = ev(V.tensor_copy(T.xq[:, 240:560].indirect(T.posS[:, 0:16]), T.x[:]))

    c_m2 = ev(V.tensor_scalar(T.m2c[:, 0:1], T.oi[:, 0:1], 2.0, None, A.is_lt))
    c_mB = ev(V.tensor_scalar(T.mB[:, 0:1], T.oi[:, 0:1], 14.0, None, A.is_ge))
    wait("s", c_B, c_m0)
    c_R0 = ev(S.activation(T.R0[:], T.Ball[:], AF.Identity, scale=T.m0[:, 0:1]))
    wait("s", c_m2)
    c_mb = ev(S.activation(T.m2b[:, 0:1], T.m2c[:, 0:1], AF.Copy))
    wait("s", c_mB)
    c_BB = ev(S.activation(T.BallB[:], T.Ball[:], AF.Identity, scale=T.mB[:, 0:1]))
    c_FK = ev(S.activation(T.FK[:], T.F[:], AF.Identity, scale=T.m2c[:, 0:1]))
    c_FB = ev(S.activation(T.FB[:], T.F[:], AF.Identity, scale=T.mB[:, 0:1]))
    c_I16 = ev(S.activation(T.Id16[:], T.Id[:], AF.Copy, scale=16.0))

    near = [r for r in range(N) if r != own and topo.die(T.cores[r]) == topo.die(core)]
    far = [r for r in range(N) if r != own and topo.die(T.cores[r]) != topo.die(core)]
    masks = {}
    for k, r in enumerate(far):
        masks[r] = topo.engines(core, T.cores[r])[0::2][4 * k:4 * k + 4]
    for k, r in enumerate(near):
        masks[r] = topo.engines(core, T.cores[r])[1::2][4 * k:4 * k + 4]

    def send(buf, sb, db, sem, lsem):
        tr = []
        for r in far + near:
            rid, pid, _s = topo.addr(T.cores[r])
            a, b = sb(r), db(r)
            tr.append(RemoteDMATransfer(dst_ids=[DstId(rid=rid, pnc=pid)], dma_engine_mask=sum(1 << e for e in masks[r]),
                                        remote_sem=sem, src=buf[:, a:a + CAP], dst=buf[:, b:b + CAP]))
        g.remote_dma_fused(tr, local_sem=lsem)

    wait("g", r_sc)
    send(T.xq, lambda r: 240 + CAP * ((r - own) % N), lambda r: CAP * ((own - r) % N - 1), T.sem.arrx, T.sem.lsx)
    a_x = ("arrx", 12)
    g.sem_inc(T.sem.sent, 1)

    wait("y", b_hi, b_lo, f1, f3, f4, *f2)
    t_b = dm(Y.dma_start(T.TB[14::16, 0:3072], T.bhi[:]))
    t_c = dm(Y.dma_start(T.TB[15::16, 0:3072], T.blo[:]))
    wait("y", k_hi, k_lo)
    t_k = dm(Y.dma_start(T.TB[0::16, :], T.khi[:]))
    t_l = dm(Y.dma_start(T.TB[1::16, :], T.klo[:]))
    e_nk.append(dm(Y.dma_start(T.nks[:, NKA:NKB], T.nk[:, NKA:NKB])))
    wait("y", ("sent", 1))
    e_nk.append(dm(Y.dma_start(T.nks[:, NKB:3072], T.nk[:, NKB:3072])))
    e_vec = dm(Y.dma_start(T.vecs[:], T.vec[:]))
    tb = [t_k, t_l, t_b, t_c]

    X = T.xq[:, 0:NS]
    wait("p", c_R0, b_hi, b_lo)
    P.matmul(T.p4[:, 0:1], T.R0[:], T.bhi[:, 0:1], True, False)
    d0 = ev(P.matmul(T.p4[:, 0:1], T.R0[:], T.blo[:, 0:1], False, True))
    wait("v", d0, c_i)
    d1 = ev(V.tensor_scalar(T.e1[:, 0:8], T.Z[:, 0:8], T.p4[:, 0:1], T.icol[:, 0:1], A.add, A.add))
    wait("v", d1, *tb)
    d2 = ev(V.tensor_tensor(T.km[:], T.TB[:].indirect(T.e1[:, 0:8]), T.Ball[:], A.mult))
    wait("p", c_mb, d2)
    d3 = ev(P.matmul(T.p5[:, 0:1], T.km[:], T.m2b[:, 0:1], True, True))
    wait("v", d3)
    d4 = ev(V.tensor_copy(T.ml2[:, 0:1], T.p5[:, 0:1]))
    wait("v", d4)
    d5 = ev(V.tensor_copy(T.bm[:], T.TB[:, 0:3072].indirect(T.ml2[:, 0:1])))
    wait("p", c_BB, d5)
    d6 = ev(P.matmul(T.p6[:, 0:16], T.BallB[:], T.bm[:], True, True))
    wait("v", r_pg)
    r_posg = ev(V.tensor_scalar(T.posG[:], T.p3[:, 0:16], -1.0, None, A.add))
    wait("v", e_nk[0])
    c_rt = ev(V.tensor_copy(T.rootc[:, 0:1], T.nks[:, 0:1]))

    def to_list(buf, ps, event, add):
        wait("v", event)
        e = ev(V.tensor_scalar(buf[:], ps[:, 0:20], float(add), None, A.add))
        wait("v", e)
        return e

    def two_lists(buf, ps, event, add):
        wait("v", event)
        return [ev(V.tensor_scalar(buf[:, 10 * p:10 * p + 10], ps[:, p:20:2], float(add), None, A.add)) for p in range(2)]

    def level(keys, starts, lst, el, ge, bp, ps, deps_v, deps_s):
        wait("s", el[0], *deps_s)
        ea = ev(S.activation(bp[:, 64:160], starts.indirect(lst[:, 4:10]), AF.Copy))
        wait("v", el[0], *deps_v, *deps_s)
        eb = ev(V.tensor_copy(bp[:, 0:64], starts.indirect(lst[:, 0:4])))
        g0 = ev(V.tensor_tensor(ge[:, 0:160], keys.indirect(lst[:, 0:10]), T.xq[:, 0:160], A.is_le))
        wait("s", el[1])
        ec = ev(S.activation(bp[:, 160:320], starts.indirect(lst[:, 10:20]), AF.Copy))
        wait("v", el[1])
        g1 = ev(V.tensor_tensor(ge[:, 160:320], keys.indirect(lst[:, 10:20]), T.xq[:, 160:320], A.is_le))
        return halves(ps, [(T.FB, bp, 0, [c_FB, ea, eb]), (T.F, ge, 0, [g0]), (T.FB, bp, 1, [ec]), (T.F, ge, 1, [g1])])

    def child(lst, el, kg, ps):
        ee = []
        for h, va in enumerate((6, 4)):
            c = 10 * h
            wait("s", el[h])
            a = ev(S.activation(kg[:, 16 * (c + va):16 * (c + 10)], T.TB[:].indirect(lst[:, c + va:c + 10]), AF.Copy))
            wait("v", el[h])
            b = ev(V.tensor_copy(kg[:, 16 * c:16 * (c + va)], T.TB[:].indirect(lst[:, c:c + va])))
            ee.append([a, b])
        return halves(ps, [(T.FK, kg, 0, [c_FK] + ee[0]), (T.FK, kg, 1, ee[1])])

    wait("v", r_sc, c_rt)
    w0 = ev(V.tensor_scalar(T.ge1[:, 240:320], T.xq[:, 240:320], T.rootc[:, 0:1], None, A.is_ge))
    wait("v", a_x)
    w1 = ev(V.tensor_scalar(T.ge1[:, 0:240], T.xq[:, 0:240], T.rootc[:, 0:1], None, A.is_ge))
    q1 = collect(T.p5, 20, [(T.F, T.ge1, True, [c_F, w0, w1])])
    wait("v", d6)
    d7 = ev(V.tensor_scalar(T.e2[:], T.p6[:, 0:16], T.icol[:, 0:1], None, A.add))
    wait("v", d7)
    d8 = ev(V.tensor_copy(T.kg3[:, 0:128], T.TB[:].indirect(T.e2[:, 0:8])))
    wait("s", d7, *tb)
    d9 = ev(S.activation(T.kg3[:, 128:256], T.TB[:].indirect(T.e2[:, 8:16]), AF.Copy))
    d10 = collect(T.p4, 16, [(T.FK, T.kg3, True, [c_FK, d8, d9])])
    wait("v", *e_nk)
    d11 = ev(V.tensor_copy(T.nk2[:], T.nks[:].indirect(T.ml2[:, 0:1])))
    s2 = to_list(T.s2, T.p5, q1, -1)
    wait("s", s2)
    s2f = ev(S.activation(T.s2f[:], T.p5[:, 0:20], AF.Copy))
    wait("v", d11)
    w2 = ev(V.tensor_tensor(T.ge2[:], T.nk2[:].indirect(T.s2[:]), X, A.is_le))
    wait("p", s2f, c_I16)
    P.matmul(T.p6[:, 0:20], T.Id16[:], T.s2f[:], True, False)
    q2 = collect(T.p6, 20, [(T.F, T.ge2, True, [w2])], False)
    wait("v", d10)
    d12 = ev(V.tensor_copy(T.ml3[:], T.p4[:, 0:16]))
    wait("s", d12)
    d14 = ev(S.activation(T.bl3[:], T.TB[:, 0:3072].indirect(T.ml3[:]), AF.Copy))
    wait("v", d12)
    d13 = ev(V.tensor_copy(T.nk3[:], T.nks[:].indirect(T.ml3[:])))
    s3 = to_list(T.s3, T.p6, q2, -17)
    e3 = two_lists(T.e3, T.p4, level(T.nk3[:], T.bl3[:], T.s3, [s3, s3], T.ge3, T.bp3, T.p4, [d13], [d14]), -1)
    n4 = two_lists(T.n4, T.p5, child(T.e3, e3, T.kg4, T.p5), 0)
    e4 = two_lists(T.e4, T.p6, level(T.nks[:], T.TB[:, 0:3072], T.n4, n4, T.ge4, T.bp4, T.p6, [], []), -1)
    n5 = two_lists(T.n5, T.p4, child(T.e4, e4, T.kg5, T.p4), 0)
    e5 = two_lists(T.e5, T.p5, level(T.nks[:], T.TB[:, 0:3072], T.n5, n5, T.ge5, T.bp5, T.p5, [], []), -1)
    vl = two_lists(T.vl, T.p6, child(T.e5, e5, T.kg6, T.p6), 0)

    wait("v", e_vec, vl[0])
    va = ev(V.tensor_copy(T.ansb[:, 0:128], T.vecs[:].indirect(T.vl[:, 0:8])))
    wait("s", e_vec, *vl)
    vb = ev(S.activation(T.ansb[:, 128:256], T.vecs[:].indirect(T.vl[:, 8:16]), AF.Copy))
    wait("v", vl[1])
    vc = ev(V.tensor_copy(T.ansb[:, 256:320], T.vecs[:].indirect(T.vl[:, 16:20])))
    wait("g", va, vb)
    send(T.ansb, lambda r: CAP * ((r - own) % N - 1), lambda r: 240 + CAP * ((own - r) % N), T.sem.arry, T.sem.lsy)
    a_y = ("arry", 12)

    wait("v", a_y, va, vb, vc, r_posg)
    wait("s", a_y, va, vb, vc, r_posg)
    y1 = ev(V.tensor_copy(T.yb[:, 0:128], T.ansb[:, 240:560].indirect(T.posG[:, 0:8])))
    y2 = ev(S.activation(T.yb[:, 128:256], T.ansb[:, 240:560].indirect(T.posG[:, 8:16]), AF.Copy))
    wait("y", y1, y2)
    st = dm(Y.dma_start(T.y[:], T.yb[:]))
    wait("y", st)
    wait("g", ("lsx", 12), ("lsy", 12))
